import numpy as np
import ml_dtypes


def mxq(x, axis, fmt="e4m3"):
    dtype, down = {"e4m3": (ml_dtypes.float8_e4m3fn, 7), "e5m2": (ml_dtypes.float8_e5m2, 14)}[fmt]
    v = np.moveaxis(np.asarray(x, np.float32).astype(ml_dtypes.bfloat16).astype(np.float64), axis, -1)
    blocks = v.reshape(v.shape[:-1] + (-1, 32))
    amax = np.abs(blocks).max(-1, keepdims=True)
    byte = np.maximum(np.where(amax > 0, np.frexp(amax)[1] - 1 + 127, 0) - down, 1)
    scale = np.exp2(byte - 127.0)
    codes = (blocks / scale).astype(np.float32).astype(dtype).astype(np.float64)
    return np.moveaxis((codes * scale).reshape(v.shape), -1, axis)


WIDE = False


def mx_kscale(k):
    if not WIDE:
        return np.ones(k)
    levels = np.array([10, -10, 5, -5, 0])
    if k % 512:
        return np.exp2(np.random.permutation(np.resize(levels, k // 32))).repeat(32)
    a = np.empty((k // 512, 16))
    for p in range(k // 512):
        a[p, :8] = np.random.permutation(np.resize(levels, 8))
        for g in range(8):
            far = levels[np.abs(levels - a[p, g]) >= 10]
            a[p, g + 8] = far[np.random.randint(len(far))]
    return np.exp2(a.ravel()).repeat(32)


def f64(x):
    return np.asarray(x).astype(np.float64)


def striped(idx):
    return np.tile(idx.reshape(-1, 16).T, (8, 1)).astype(np.uint16)


def unstriped(offs):
    return offs[:16].T.reshape(-1).astype(np.int64)


E2M1 = np.array([0.0, 0.5, 1.0, 1.5, 2.0, 3.0, 4.0, 6.0, -0.0, -0.5, -1.0, -1.5, -2.0, -3.0, -4.0, -6.0])


def pack_weight(w, fmt):
    k, n = w.shape
    w = f64(np.asarray(w, np.float32).astype(ml_dtypes.bfloat16)).reshape(k // 32, 32, n)
    amax = np.abs(w).max(1)
    if fmt == "e4m3":
        byte = np.frexp(amax)[1] - 1 + 127 - 7
    else:
        mant, ex = np.frexp(amax / 6.0)
        byte = np.where(mant > 0.5, ex, ex - 1) + 127
    byte = np.clip(np.where(amax > 0, byte, 1), 1, 254)
    scaled = (w * np.exp2(127.0 - byte)[:, None, :]).reshape(k, n).astype(np.float32)
    by_word = np.ascontiguousarray(scaled.reshape(k // 512, 128, 4, n).transpose(0, 1, 3, 2))
    if fmt == "e4m3":
        words = by_word.astype(ml_dtypes.float8_e4m3fn).view(np.uint8)
    else:
        c = by_word.astype(ml_dtypes.float4_e2m1fn).view(np.uint8) & 0xF
        words = (c[..., 0::2] | (c[..., 1::2] << 4)).reshape(k // 512, 128, 2 * n)
    return np.ascontiguousarray(words), np.ascontiguousarray(byte.astype(np.uint8).reshape(k // 512, 16, n))


def unpack_weight(words, scales, fmt):
    g, _, n = scales.shape
    words = np.ascontiguousarray(words).reshape(g, 128, n, -1)
    if fmt == "e4m3":
        vals = words.view(ml_dtypes.float8_e4m3fn).astype(np.float64)
    else:
        nib = np.empty((g, 128, n, 4), np.uint8)
        nib[..., 0::2] = words & 0xF
        nib[..., 1::2] = words >> 4
        vals = E2M1[nib]
    vals = vals * np.repeat(np.exp2(scales.astype(np.float64) - 127.0), 8, axis=1)[..., None]
    return vals.transpose(0, 1, 3, 2).reshape(g * 512, n)


def pack_table(v):
    words, scales = pack_weight(v, "e4m3")
    return np.concatenate([words.reshape(words.shape[0], -1), scales.reshape(scales.shape[0], -1)], axis=1)


def unpack_table(tab):
    g, t = tab.shape[0], tab.shape[1] // 528
    return unpack_weight(tab[:, :512 * t].reshape(g, 128, t, 4), tab[:, 512 * t:].reshape(g, 16, t), "e4m3")


def silu(v):
    return v / (1.0 + np.exp(-np.maximum(v, -700.0)))


K, M, T, S = 2048, 128, 2048, 512


def setup_inputs():
    n = np.random.standard_normal
    s = mx_kscale(K)[:, None]
    return {
        "tab": pack_table(n((K, T)) * s),
        "w": (n((K, M)) / np.sqrt(K) / s).astype(np.float32),
        "b": (0.3 * n(128)).astype(np.float32),
        "offs": striped(np.random.permutation(T)[:S]),
    }


def reference(tab, w, b, offs):
    tab_ = unpack_table(tab)[:, unstriped(offs)]
    w_ = mxq(f64(w), 0, "e4m3")
    y = w_.T @ tab_
    return silu(y + f64(b)[:, None])

@@ -1,0 +1,84 @@
+from contextlib import ExitStack
+
+import concourse.mybir as mybir
+
+K, M, T, S = 2048, 128, 2048, 512
+P = 128
+PASSES = 4
+HALF = 256
+FLOPS = 2 * K * M * S
+
+F32 = mybir.dt.float32
+BF16 = mybir.dt.bfloat16
+I32 = mybir.dt.int32
+U32 = mybir.dt.uint32
+U16 = mybir.dt.uint16
+U8 = mybir.dt.uint8
+FP8X4 = mybir.dt.float8_e4m3fn_x4
+SILU = mybir.ActivationFunctionType.Silu
+
+
+def tile_list_tabw_silu_kernel(tc, tab, w, b, offs, out):
+    nc = tc.nc
+    with ExitStack() as ctx:
+        held = ctx.enter_context(tc.tile_pool(name="held", bufs=1))
+        psum = ctx.enter_context(tc.psum_pool(name="psum", bufs=1))
+
+        offsets = held.tile([P, S // 16], U16, name="offsets")
+        packed = held.tile([P, T // 4], I32, name="packed", align_bytes=64)
+        bias = held.tile([P, 1], F32, name="bias")
+        warm = held.tile([P, 1], F32, name="warm")
+        warmed = held.tile([P, 1], F32, name="warmed")
+        words = [held.tile([P, T], I32, name=f"words{a}", align_bytes=64) for a in range(PASSES)]
+        picked = [held.tile([P, S], U32, name=f"picked{a}", align_bytes=64) for a in range(PASSES)]
+        picked_scales = held.tile([P, S], U8, name="picked_scales", align_bytes=64)
+        acc = [psum.tile([P, HALF], F32, name=f"acc{h}") for h in range(2)]
+        result = [held.tile([P, HALF], F32, name=f"result{h}", align_bytes=64) for h in range(2)]
+
+        raw = [held.tile([P, 4, M], F32, name=f"raw{a}", align_bytes=64) for a in range(PASSES)]
+        grouped = [held.tile([P, M, 4], BF16, name=f"grouped{a}", align_bytes=64) for a in range(PASSES)]
+        codes = [held.tile([P, M], U32, name=f"codes{a}", align_bytes=64) for a in range(PASSES)]
+        scales = [held.tile([P, M], U8, name=f"scales{a}", align_bytes=64) for a in range(PASSES)]
+
+        nc.vector.memset(packed[:], 0)
+        nc.vector.memset(warm[:], 0.0)
+        scale_rows = tab[:, 512 * T : 528 * T].bitcast(I32).rearrange("a (q t) -> a q t", q=16)
+        for quad in range(4):
+            nc.scalar.dma_start(packed[32 * quad : 32 * quad + 16, :], scale_rows[:, 4 * quad : 4 * quad + 4, :])
+        nc.sync.dma_start(offsets[:], offs)
+        for a in range(PASSES):
+            nc.sync.dma_start(words[a][:], tab[a, 0 : 512 * T].bitcast(I32).rearrange("(p t) -> p t", p=P))
+        for a in range(PASSES):
+            nc.sync.dma_start(raw[a][:], w[512 * a : 512 * (a + 1), :].rearrange("(p j) n -> p j n", j=4))
+        nc.sync.dma_start(bias[:], b.rearrange("(p o) -> p o", o=1))
+        nc.scalar.activation(warmed[:], warm[:], SILU)
+
+        def multiply(a, h):
+            cols = slice(h * HALF, (h + 1) * HALF)
+            nc.tensor.matmul_mx(
+                out=acc[h][:],
+                lhsT=codes[a][:].bitcast(FP8X4),
+                lhsT_scale=scales[a][:],
+                rhs=picked[a][:, cols].bitcast(FP8X4),
+                rhs_scale=picked_scales[4 * a :, cols],
+                start=(a == 0),
+                stop=(a == PASSES - 1),
+            )
+
+        for a in range(PASSES):
+            nc.vector.tensor_copy(picked[a][:], words[a][:].bitcast(U32).indirect(offsets[:]))
+            if a == 0:
+                nc.vector.tensor_copy(picked_scales[:], packed[:].bitcast(U8).indirect(offsets[:]))
+        for a in range(PASSES):
+            src, dst = raw[a][:].rearrange("p j n -> p n j"), grouped[a][:]
+            if a in (0, 1, 2):
+                nc.scalar.copy(dst, src)
+            else:
+                nc.vector.tensor_copy(dst, src)
+            nc.vector.quantize_mx(out=codes[a][:].bitcast(FP8X4), scales=scales[a][:], in_=grouped[a][:].rearrange("p n j -> p (n j)"))
+            for h in range(2):
+                multiply(a, h)
+
+        for h in range(2):
+            nc.scalar.activation(result[h][:], acc[h][:], SILU, bias=bias[:])
+            nc.sync.dma_start(out[:, h * HALF : (h + 1) * HALF], result[h][:])

@@ -35,7 +35,7 @@ def tile_list_tabw_silu_kernel(tc, tab, w, b, offs, out):
         acc = [psum.tile([P, HALF], F32, name=f"acc{h}") for h in range(2)]
         result = [held.tile([P, HALF], F32, name=f"result{h}", align_bytes=64) for h in range(2)]
 
-        raw = [held.tile([P, 4, M], F32, name=f"raw{a}", align_bytes=64) for a in range(PASSES)]
+        raw = held.tile([P, PASSES, 4, M], F32, name="raw", align_bytes=64)
         grouped = [held.tile([P, M, 4], BF16, name=f"grouped{a}", align_bytes=64) for a in range(PASSES)]
         codes = [held.tile([P, M], U32, name=f"codes{a}", align_bytes=64) for a in range(PASSES)]
         scales = [held.tile([P, M], U8, name=f"scales{a}", align_bytes=64) for a in range(PASSES)]
@@ -43,13 +43,12 @@ def tile_list_tabw_silu_kernel(tc, tab, w, b, offs, out):
         nc.vector.memset(packed[:], 0)
         nc.vector.memset(warm[:], 0.0)
         scale_rows = tab[:, 512 * T : 528 * T].bitcast(I32).rearrange("a (q t) -> a q t", q=16)
-        for quad in range(4):
-            nc.scalar.dma_start(packed[32 * quad : 32 * quad + 16, :], scale_rows[:, 4 * quad : 4 * quad + 4, :])
+        nc.sync.dma_start(raw[:].rearrange("p a j n -> p a (j n)"), w.rearrange("(a p j) n -> p a (j n)", p=P, j=4))
         nc.sync.dma_start(offsets[:], offs)
+        for quad in range(4):
+            nc.sync.dma_start(packed[32 * quad : 32 * quad + 16, :], scale_rows[:, 4 * quad : 4 * quad + 4, :])
         for a in range(PASSES):
             nc.sync.dma_start(words[a][:], tab[a, 0 : 512 * T].bitcast(I32).rearrange("(p t) -> p t", p=P))
-        for a in range(PASSES):
-            nc.sync.dma_start(raw[a][:], w[512 * a : 512 * (a + 1), :].rearrange("(p j) n -> p j n", j=4))
         nc.sync.dma_start(bias[:], b.rearrange("(p o) -> p o", o=1))
         nc.scalar.activation(warmed[:], warm[:], SILU)
 
@@ -65,18 +64,18 @@ def tile_list_tabw_silu_kernel(tc, tab, w, b, offs, out):
                 stop=(a == PASSES - 1),
             )
 
+        nc.vector.tensor_copy(picked_scales[:], packed[:].bitcast(U8).indirect(offsets[:]))
         for a in range(PASSES):
-            nc.vector.tensor_copy(picked[a][:], words[a][:].bitcast(U32).indirect(offsets[:]))
-            if a == 0:
-                nc.vector.tensor_copy(picked_scales[:], packed[:].bitcast(U8).indirect(offsets[:]))
-        for a in range(PASSES):
-            src, dst = raw[a][:].rearrange("p j n -> p n j"), grouped[a][:]
-            if a in (0, 1, 2):
-                nc.scalar.copy(dst, src)
-            else:
-                nc.vector.tensor_copy(dst, src)
+            nc.scalar.copy(grouped[a][:], raw[:, a].rearrange("p j n -> p n j"))
             nc.vector.quantize_mx(out=codes[a][:].bitcast(FP8X4), scales=scales[a][:], in_=grouped[a][:].rearrange("p n j -> p (n j)"))
+        for a in range(PASSES):
+            window = words[a][:].bitcast(U32)
+            if a < PASSES - 1:
+                nc.vector.tensor_copy(picked[a][:], window.indirect(offsets[:]))
             for h in range(2):
+                if a == PASSES - 1:
+                    cols = slice(h * HALF, (h + 1) * HALF)
+                    nc.vector.tensor_copy(picked[a][:, cols], window.indirect(offsets[:, h * HALF // 16 : (h + 1) * HALF // 16]))
                 multiply(a, h)
 
         for h in range(2):

@@ -29,9 +29,8 @@ def tile_list_tabw_silu_kernel(tc, tab, w, b, offs, out):
         bias = held.tile([P, 1], F32, name="bias")
         warm = held.tile([P, 1], F32, name="warm")
         warmed = held.tile([P, 1], F32, name="warmed")
-        words = [held.tile([P, T], I32, name=f"words{a}", align_bytes=64) for a in range(PASSES)]
+        words = [held.tile([P, T], I32, name=f"words{a}", tag=f"words{a}", align_bytes=64) for a in range(PASSES)]
         picked = [held.tile([P, S], U32, name=f"picked{a}", align_bytes=64) for a in range(PASSES)]
-        picked_scales = held.tile([P, S], U8, name="picked_scales", align_bytes=64)
         acc = [psum.tile([P, HALF], F32, name=f"acc{h}") for h in range(2)]
         result = [held.tile([P, HALF], F32, name=f"result{h}", align_bytes=64) for h in range(2)]
 
@@ -46,7 +45,7 @@ def tile_list_tabw_silu_kernel(tc, tab, w, b, offs, out):
         nc.sync.dma_start(raw[:].rearrange("p a j n -> p a (j n)"), w.rearrange("(a p j) n -> p a (j n)", p=P, j=4))
         nc.sync.dma_start(offsets[:], offs)
         for quad in range(4):
-            nc.sync.dma_start(packed[32 * quad : 32 * quad + 16, :], scale_rows[:, 4 * quad : 4 * quad + 4, :])
+            nc.gpsimd.dma_start(packed[32 * quad : 32 * quad + 16, :], scale_rows[:, 4 * quad : 4 * quad + 4, :])
         for a in range(PASSES):
             nc.sync.dma_start(words[a][:], tab[a, 0 : 512 * T].bitcast(I32).rearrange("(p t) -> p t", p=P))
         nc.sync.dma_start(bias[:], b.rearrange("(p o) -> p o", o=1))
@@ -64,13 +63,16 @@ def tile_list_tabw_silu_kernel(tc, tab, w, b, offs, out):
                 stop=(a == PASSES - 1),
             )
 
-        nc.vector.tensor_copy(picked_scales[:], packed[:].bitcast(U8).indirect(offsets[:]))
         for a in range(PASSES):
             nc.scalar.copy(grouped[a][:], raw[:, a].rearrange("p j n -> p n j"))
             nc.vector.quantize_mx(out=codes[a][:].bitcast(FP8X4), scales=scales[a][:], in_=grouped[a][:].rearrange("p n j -> p (n j)"))
+        for a in range(2):
+            nc.vector.tensor_copy(picked[a][:], words[a][:].bitcast(U32).indirect(offsets[:]))
+        picked_scales = held.tile([P, S], U8, name="picked_scales", tag="words1", align_bytes=64)
+        nc.vector.tensor_copy(picked_scales[:], packed[:].bitcast(U8).indirect(offsets[:]))
         for a in range(PASSES):
             window = words[a][:].bitcast(U32)
-            if a < PASSES - 1:
+            if a == 2:
                 nc.vector.tensor_copy(picked[a][:], window.indirect(offsets[:]))
             for h in range(2):
                 if a == PASSES - 1:

@@ -6,6 +6,7 @@ K, M, T, S = 2048, 128, 2048, 512
 P = 128
 PASSES = 4
 HALF = 256
+PIECE = 128
 FLOPS = 2 * K * M * S
 
 F32 = mybir.dt.float32
@@ -31,8 +32,8 @@ def tile_list_tabw_silu_kernel(tc, tab, w, b, offs, out):
         warmed = held.tile([P, 1], F32, name="warmed")
         words = [held.tile([P, T], I32, name=f"words{a}", tag=f"words{a}", align_bytes=64) for a in range(PASSES)]
         picked = [held.tile([P, S], U32, name=f"picked{a}", align_bytes=64) for a in range(PASSES)]
-        acc = [psum.tile([P, HALF], F32, name=f"acc{h}") for h in range(2)]
-        result = [held.tile([P, HALF], F32, name=f"result{h}", align_bytes=64) for h in range(2)]
+        acc = [psum.tile([P, PIECE], F32, name=f"acc{c}") for c in range(S // PIECE)]
+        result = [held.tile([P, PIECE], F32, name=f"result{c}", align_bytes=64) for c in range(S // PIECE)]
 
         raw = held.tile([P, PASSES, 4, M], F32, name="raw", align_bytes=64)
         grouped = [held.tile([P, M, 4], BF16, name=f"grouped{a}", align_bytes=64) for a in range(PASSES)]
@@ -51,10 +52,10 @@ def tile_list_tabw_silu_kernel(tc, tab, w, b, offs, out):
         nc.sync.dma_start(bias[:], b.rearrange("(p o) -> p o", o=1))
         nc.scalar.activation(warmed[:], warm[:], SILU)
 
-        def multiply(a, h):
-            cols = slice(h * HALF, (h + 1) * HALF)
+        def multiply(a, c):
+            cols = slice(c * PIECE, (c + 1) * PIECE)
             nc.tensor.matmul_mx(
-                out=acc[h][:],
+                out=acc[c][:],
                 lhsT=codes[a][:].bitcast(FP8X4),
                 lhsT_scale=scales[a][:],
                 rhs=picked[a][:, cols].bitcast(FP8X4),
@@ -78,8 +79,9 @@ def tile_list_tabw_silu_kernel(tc, tab, w, b, offs, out):
                 if a == PASSES - 1:
                     cols = slice(h * HALF, (h + 1) * HALF)
                     nc.vector.tensor_copy(picked[a][:, cols], window.indirect(offsets[:, h * HALF // 16 : (h + 1) * HALF // 16]))
-                multiply(a, h)
+                for c in (2 * h, 2 * h + 1):
+                    multiply(a, c)
 
-        for h in range(2):
-            nc.scalar.activation(result[h][:], acc[h][:], SILU, bias=bias[:])
-            nc.sync.dma_start(out[:, h * HALF : (h + 1) * HALF], result[h][:])
+        for c in range(S // PIECE):
+            nc.scalar.activation(result[c][:], acc[c][:], SILU, bias=bias[:])
+            nc.sync.dma_start(out[:, c * PIECE : (c + 1) * PIECE], result[c][:])

@@ -1,6 +1,7 @@
 from contextlib import ExitStack
 
 import concourse.mybir as mybir
+from concourse.masks import make_identity
 
 K, M, T, S = 2048, 128, 2048, 512
 P = 128
@@ -26,24 +27,30 @@ def tile_list_tabw_silu_kernel(tc, tab, w, b, offs, out):
         psum = ctx.enter_context(tc.psum_pool(name="psum", bufs=1))
 
         offsets = held.tile([P, S // 16], U16, name="offsets")
-        packed = held.tile([P, T // 4], I32, name="packed", align_bytes=64)
+        packed = held.tile([P, T // 4], I32, name="packed", tag="packed", align_bytes=64)
         bias = held.tile([P, 1], F32, name="bias")
         warm = held.tile([P, 1], F32, name="warm")
         warmed = held.tile([P, 1], F32, name="warmed")
         words = [held.tile([P, T], I32, name=f"words{a}", tag=f"words{a}", align_bytes=64) for a in range(PASSES)]
-        picked = [held.tile([P, S], U32, name=f"picked{a}", align_bytes=64) for a in range(PASSES)]
+        picked = {a: held.tile([P, S], U32, name=f"picked{a}", align_bytes=64) for a in (0, 1, 3)}
         acc = [psum.tile([P, PIECE], F32, name=f"acc{c}") for c in range(S // PIECE)]
         result = [held.tile([P, PIECE], F32, name=f"result{c}", align_bytes=64) for c in range(S // PIECE)]
 
-        raw = held.tile([P, PASSES, 4, M], F32, name="raw", align_bytes=64)
-        grouped = [held.tile([P, M, 4], BF16, name=f"grouped{a}", align_bytes=64) for a in range(PASSES)]
-        codes = [held.tile([P, M], U32, name=f"codes{a}", align_bytes=64) for a in range(PASSES)]
-        scales = [held.tile([P, M], U8, name=f"scales{a}", align_bytes=64) for a in range(PASSES)]
+        raw = held.tile([P, 8, 2, M], F32, name="raw", align_bytes=64)
+        pairs = [held.tile([P, 4, M, 2], BF16, name=f"pairs{g}", align_bytes=64) for g in range(2)]
+        turned = held.tile([P, P, 8], F32, name="turned", align_bytes=64)
+        ident = held.tile([P, P], F32, name="ident", align_bytes=64)
+        first = [psum.tile([P, 4, P], F32, name=f"first{g}") for g in range(2)]
+        second = [psum.tile([P, 2, 2, M], F32, name=f"second{g}") for g in range(2)]
+        grouped = [held.tile([P, 2, M, 4], BF16, name=f"grouped{g}", align_bytes=64) for g in range(2)]
+        codes = [held.tile([P, 2, M], U32, name=f"codes{g}", align_bytes=64) for g in range(2)]
+        scales = [held.tile([P, 2, M], U8, name=f"scales{g}", align_bytes=64) for g in range(2)]
 
+        make_identity(nc, ident[:])
         nc.vector.memset(packed[:], 0)
         nc.vector.memset(warm[:], 0.0)
         scale_rows = tab[:, 512 * T : 528 * T].bitcast(I32).rearrange("a (q t) -> a q t", q=16)
-        nc.sync.dma_start(raw[:].rearrange("p a j n -> p a (j n)"), w.rearrange("(a p j) n -> p a (j n)", p=P, j=4))
+        nc.sync.dma_start(raw[:].rearrange("p r e n -> p (r e n)"), w.rearrange("(p r) n -> p (r n)", p=P))
         nc.sync.dma_start(offsets[:], offs)
         for quad in range(4):
             nc.gpsimd.dma_start(packed[32 * quad : 32 * quad + 16, :], scale_rows[:, 4 * quad : 4 * quad + 4, :])
@@ -56,21 +63,38 @@ def tile_list_tabw_silu_kernel(tc, tab, w, b, offs, out):
             cols = slice(c * PIECE, (c + 1) * PIECE)
             nc.tensor.matmul_mx(
                 out=acc[c][:],
-                lhsT=codes[a][:].bitcast(FP8X4),
-                lhsT_scale=scales[a][:],
+                lhsT=codes[a // 2][:, a % 2].bitcast(FP8X4),
+                lhsT_scale=scales[a // 2][:, a % 2],
                 rhs=picked[a][:, cols].bitcast(FP8X4),
                 rhs_scale=picked_scales[4 * a :, cols],
                 start=(a == 0),
                 stop=(a == PASSES - 1),
             )
 
-        for a in range(PASSES):
-            nc.scalar.copy(grouped[a][:], raw[:, a].rearrange("p j n -> p n j"))
-            nc.vector.quantize_mx(out=codes[a][:].bitcast(FP8X4), scales=scales[a][:], in_=grouped[a][:].rearrange("p n j -> p (n j)"))
+        for g in range(2):
+            nc.vector.tensor_copy(pairs[g][:], raw[:, 4 * g : 4 * g + 4].rearrange("p r e n -> p r n e"))
+            pair_words = pairs[g][:].rearrange("p r n e -> p r (n e)").bitcast(F32)
+            for r in range(4):
+                nc.tensor.transpose(first[g][:, r], pair_words[:, r], ident[:])
+            nc.scalar.copy(turned[:, :, 4 * g : 4 * g + 4], first[g][:].rearrange("n r p -> n p r"))
+        turned_row = turned[:].rearrange("n p r -> n (p r)")
+        for g in range(2):
+            for a in range(2):
+                for u in range(2):
+                    start = 256 * (2 * g + a)
+                    nc.tensor.transpose(second[g][:, a, u], turned_row[:, start + u : start + 256 : 2], ident[:])
+            grouped_words = grouped[g][:].rearrange("p a n j -> p (a n j)").bitcast(F32).rearrange("p (a n u) -> p a n u", a=2, u=2)
+            nc.scalar.copy(grouped_words, second[g][:].rearrange("p a u n -> p a n u"))
+            nc.vector.quantize_mx(
+                out=codes[g][:].rearrange("p a n -> p (a n)").bitcast(FP8X4),
+                scales=scales[g][:].rearrange("p a n -> p (a n)"),
+                in_=grouped[g][:].rearrange("p a n j -> p (a n j)"),
+            )
         for a in range(2):
             nc.vector.tensor_copy(picked[a][:], words[a][:].bitcast(U32).indirect(offsets[:]))
         picked_scales = held.tile([P, S], U8, name="picked_scales", tag="words1", align_bytes=64)
         nc.vector.tensor_copy(picked_scales[:], packed[:].bitcast(U8).indirect(offsets[:]))
+        picked[2] = held.tile([P, S], U32, name="picked2", tag="packed", align_bytes=64)
         for a in range(PASSES):
             window = words[a][:].bitcast(U32)
             if a == 2:

@@ -36,9 +36,9 @@ def tile_list_tabw_silu_kernel(tc, tab, w, b, offs, out):
         acc = [psum.tile([P, PIECE], F32, name=f"acc{c}") for c in range(S // PIECE)]
         result = [held.tile([P, PIECE], F32, name=f"result{c}", align_bytes=64) for c in range(S // PIECE)]
 
-        raw = held.tile([P, 8, 2, M], F32, name="raw", align_bytes=64)
+        raw = held.tile([P, 4, 2, 2, M], F32, name="raw", align_bytes=64)
         pairs = [held.tile([P, 4, M, 2], BF16, name=f"pairs{g}", align_bytes=64) for g in range(2)]
-        turned = held.tile([P, P, 8], F32, name="turned", align_bytes=64)
+        turned = [held.tile([P, P, 4], F32, name=f"turned{u}", align_bytes=64) for u in range(2)]
         ident = held.tile([P, P], F32, name="ident", align_bytes=64)
         first = [psum.tile([P, 4, P], F32, name=f"first{g}") for g in range(2)]
         second = [psum.tile([P, 2, 2, M], F32, name=f"second{g}") for g in range(2)]
@@ -50,7 +50,7 @@ def tile_list_tabw_silu_kernel(tc, tab, w, b, offs, out):
         nc.vector.memset(packed[:], 0)
         nc.vector.memset(warm[:], 0.0)
         scale_rows = tab[:, 512 * T : 528 * T].bitcast(I32).rearrange("a (q t) -> a q t", q=16)
-        nc.sync.dma_start(raw[:].rearrange("p r e n -> p (r e n)"), w.rearrange("(p r) n -> p (r n)", p=P))
+        nc.sync.dma_start(raw[:].rearrange("p c u e n -> p (c u e n)"), w.rearrange("(p r) n -> p (r n)", p=P))
         nc.sync.dma_start(offsets[:], offs)
         for quad in range(4):
             nc.gpsimd.dma_start(packed[32 * quad : 32 * quad + 16, :], scale_rows[:, 4 * quad : 4 * quad + 4, :])
@@ -72,17 +72,17 @@ def tile_list_tabw_silu_kernel(tc, tab, w, b, offs, out):
             )
 
         for g in range(2):
-            nc.vector.tensor_copy(pairs[g][:], raw[:, 4 * g : 4 * g + 4].rearrange("p r e n -> p r n e"))
+            nc.vector.tensor_copy(pairs[g][:], raw[:, :, g].rearrange("p c e n -> p c n e"))
             pair_words = pairs[g][:].rearrange("p r n e -> p r (n e)").bitcast(F32)
             for r in range(4):
                 nc.tensor.transpose(first[g][:, r], pair_words[:, r], ident[:])
-            nc.scalar.copy(turned[:, :, 4 * g : 4 * g + 4], first[g][:].rearrange("n r p -> n p r"))
-        turned_row = turned[:].rearrange("n p r -> n (p r)")
+            nc.scalar.copy(turned[g][:], first[g][:].rearrange("n r p -> n p r"))
         for g in range(2):
-            for a in range(2):
-                for u in range(2):
-                    start = 256 * (2 * g + a)
-                    nc.tensor.transpose(second[g][:, a, u], turned_row[:, start + u : start + 256 : 2], ident[:])
+            for u in range(2):
+                turned_row = turned[u][:].rearrange("n p c -> n (p c)")
+                for a in range(2):
+                    start = P * (2 * g + a)
+                    nc.tensor.transpose(second[g][:, a, u], turned_row[:, start : start + P], ident[:])
             grouped_words = grouped[g][:].rearrange("p a n j -> p (a n j)").bitcast(F32).rearrange("p (a n u) -> p a n u", a=2, u=2)
             nc.scalar.copy(grouped_words, second[g][:].rearrange("p a u n -> p a n u"))
             nc.vector.quantize_mx(

@@ -24,19 +24,19 @@ def tile_list_tabw_silu_kernel(tc, tab, w, b, offs, out):
     nc = tc.nc
     with ExitStack() as ctx:
         held = ctx.enter_context(tc.tile_pool(name="held", bufs=1))
+        laid = ctx.enter_context(tc.tile_pool(name="laid", bufs=1))
         psum = ctx.enter_context(tc.psum_pool(name="psum", bufs=1))
 
         offsets = held.tile([P, S // 16], U16, name="offsets")
         packed = held.tile([P, T // 4], I32, name="packed", tag="packed", align_bytes=64)
-        bias = held.tile([P, 1], F32, name="bias")
         warm = held.tile([P, 1], F32, name="warm")
         warmed = held.tile([P, 1], F32, name="warmed")
-        words = [held.tile([P, T], I32, name=f"words{a}", tag=f"words{a}", align_bytes=64) for a in range(PASSES)]
+        words = [held.tile([P, T], I32, name=f"words{a}", tag=f"words{a}", align_bytes=64) for a in range(2)]
         picked = {a: held.tile([P, S], U32, name=f"picked{a}", align_bytes=64) for a in (0, 1, 3)}
         acc = [psum.tile([P, PIECE], F32, name=f"acc{c}") for c in range(S // PIECE)]
         result = [held.tile([P, PIECE], F32, name=f"result{c}", align_bytes=64) for c in range(S // PIECE)]
 
-        raw = held.tile([P, 4, 2, 2, M], F32, name="raw", align_bytes=64)
+        raw = laid.tile([P, 4, 2, 2, M], F32, name="raw", align_bytes=64, offset=8128)
         pairs = [held.tile([P, 4, M, 2], BF16, name=f"pairs{g}", align_bytes=64) for g in range(2)]
         turned = [held.tile([P, P, 4], F32, name=f"turned{u}", align_bytes=64) for u in range(2)]
         ident = held.tile([P, P], F32, name="ident", align_bytes=64)
@@ -54,9 +54,12 @@ def tile_list_tabw_silu_kernel(tc, tab, w, b, offs, out):
         nc.sync.dma_start(offsets[:], offs)
         for quad in range(4):
             nc.gpsimd.dma_start(packed[32 * quad : 32 * quad + 16, :], scale_rows[:, 4 * quad : 4 * quad + 4, :])
-        for a in range(PASSES):
+
+        def load_words(a):
             nc.sync.dma_start(words[a][:], tab[a, 0 : 512 * T].bitcast(I32).rearrange("(p t) -> p t", p=P))
-        nc.sync.dma_start(bias[:], b.rearrange("(p o) -> p o", o=1))
+
+        for a in range(2):
+            load_words(a)
         nc.scalar.activation(warmed[:], warm[:], SILU)
 
         def multiply(a, c):
@@ -77,6 +80,11 @@ def tile_list_tabw_silu_kernel(tc, tab, w, b, offs, out):
             for r in range(4):
                 nc.tensor.transpose(first[g][:, r], pair_words[:, r], ident[:])
             nc.scalar.copy(turned[g][:], first[g][:].rearrange("n r p -> n p r"))
+        for a in (2, 3):
+            words.append(laid.tile([P, T], I32, name=f"words{a}", align_bytes=64, offset=16256 * (a - 2)))
+            load_words(a)
+        bias = laid.tile([P, 1], F32, name="bias", align_bytes=64, offset=12288)
+        nc.sync.dma_start(bias[:], b.rearrange("(p o) -> p o", o=1))
         for g in range(2):
             for u in range(2):
                 turned_row = turned[u][:].rearrange("n p c -> n (p c)")

@@ -1,7 +1,6 @@
 from contextlib import ExitStack
 
 import concourse.mybir as mybir
-from concourse.masks import make_identity
 
 K, M, T, S = 2048, 128, 2048, 512
 P = 128
@@ -28,39 +27,28 @@ def tile_list_tabw_silu_kernel(tc, tab, w, b, offs, out):
         psum = ctx.enter_context(tc.psum_pool(name="psum", bufs=1))
 
         offsets = held.tile([P, S // 16], U16, name="offsets")
-        packed = held.tile([P, T // 4], I32, name="packed", tag="packed", align_bytes=64)
         warm = held.tile([P, 1], F32, name="warm")
         warmed = held.tile([P, 1], F32, name="warmed")
-        words = [held.tile([P, T], I32, name=f"words{a}", tag=f"words{a}", align_bytes=64) for a in range(2)]
-        picked = {a: held.tile([P, S], U32, name=f"picked{a}", align_bytes=64) for a in (0, 1, 3)}
+        planes = held.tile([P, S // 4], I32, name="planes", align_bytes=64)
         acc = [psum.tile([P, PIECE], F32, name=f"acc{c}") for c in range(S // PIECE)]
         result = [held.tile([P, PIECE], F32, name=f"result{c}", align_bytes=64) for c in range(S // PIECE)]
-
-        raw = laid.tile([P, 4, 2, 2, M], F32, name="raw", align_bytes=64, offset=8128)
-        pairs = [held.tile([P, 4, M, 2], BF16, name=f"pairs{g}", align_bytes=64) for g in range(2)]
-        turned = [held.tile([P, P, 4], F32, name=f"turned{u}", align_bytes=64) for u in range(2)]
-        ident = held.tile([P, P], F32, name="ident", align_bytes=64)
-        first = [psum.tile([P, 4, P], F32, name=f"first{g}") for g in range(2)]
-        second = [psum.tile([P, 2, 2, M], F32, name=f"second{g}") for g in range(2)]
         grouped = [held.tile([P, 2, M, 4], BF16, name=f"grouped{g}", align_bytes=64) for g in range(2)]
         codes = [held.tile([P, 2, M], U32, name=f"codes{g}", align_bytes=64) for g in range(2)]
         scales = [held.tile([P, 2, M], U8, name=f"scales{g}", align_bytes=64) for g in range(2)]
 
-        make_identity(nc, ident[:])
-        nc.vector.memset(packed[:], 0)
-        nc.vector.memset(warm[:], 0.0)
-        scale_rows = tab[:, 512 * T : 528 * T].bitcast(I32).rearrange("a (q t) -> a q t", q=16)
-        nc.sync.dma_start(raw[:].rearrange("p c u e n -> p (c u e n)"), w.rearrange("(p r) n -> p (r n)", p=P))
-        nc.sync.dma_start(offsets[:], offs)
-        for quad in range(4):
-            nc.gpsimd.dma_start(packed[32 * quad : 32 * quad + 16, :], scale_rows[:, 4 * quad : 4 * quad + 4, :])
+        raw = held.tile([P, PASSES, 4, M], F32, name="raw", tag="raw", align_bytes=64)
+        rows = laid.tile([P, T // 4], I32, name="rows", align_bytes=64, offset=2048)
+        words = {0: held.tile([P, T], I32, name="words0", tag="words0", align_bytes=64)}
+        words[1] = held.tile([P, T], I32, name="words1", tag="words1", align_bytes=64)
+        picked = {a: held.tile([P, S], U32, name=f"picked{a}", align_bytes=64) for a in (0, 3)}
 
         def load_words(a):
             nc.sync.dma_start(words[a][:], tab[a, 0 : 512 * T].bitcast(I32).rearrange("(p t) -> p t", p=P))
 
-        for a in range(2):
-            load_words(a)
-        nc.scalar.activation(warmed[:], warm[:], SILU)
+        def gather_words(a, h=None):
+            cols = slice(0, S) if h is None else slice(h * HALF, (h + 1) * HALF)
+            listed = offsets[:, cols.start // 16 : cols.stop // 16]
+            nc.vector.tensor_copy(picked[a][:, cols], words[a][:].bitcast(U32).indirect(listed))
 
         def multiply(a, c):
             cols = slice(c * PIECE, (c + 1) * PIECE)
@@ -69,48 +57,54 @@ def tile_list_tabw_silu_kernel(tc, tab, w, b, offs, out):
                 lhsT=codes[a // 2][:, a % 2].bitcast(FP8X4),
                 lhsT_scale=scales[a // 2][:, a % 2],
                 rhs=picked[a][:, cols].bitcast(FP8X4),
-                rhs_scale=picked_scales[4 * a :, cols],
+                rhs_scale=planes[:].bitcast(U8)[4 * a :, cols],
                 start=(a == 0),
                 stop=(a == PASSES - 1),
             )
 
-        for g in range(2):
-            nc.vector.tensor_copy(pairs[g][:], raw[:, :, g].rearrange("p c e n -> p c n e"))
-            pair_words = pairs[g][:].rearrange("p r n e -> p r (n e)").bitcast(F32)
-            for r in range(4):
-                nc.tensor.transpose(first[g][:, r], pair_words[:, r], ident[:])
-            nc.scalar.copy(turned[g][:], first[g][:].rearrange("n r p -> n p r"))
-        for a in (2, 3):
-            words.append(laid.tile([P, T], I32, name=f"words{a}", align_bytes=64, offset=16256 * (a - 2)))
+        scale_rows = tab[:, 512 * T : 528 * T].bitcast(I32).rearrange("a (q t) -> a q t", q=16)
+        nc.sync.dma_start(raw[:].rearrange("p a j n -> p a (j n)"), w.rearrange("(a p j) n -> p a (j n)", p=P, j=4))
+        nc.sync.dma_start(offsets[:], offs)
+        for quad in range(4):
+            first = 64 * (quad // 2) + 16 * (quad % 2)
+            nc.gpsimd.dma_start(rows[first : first + 16, :], scale_rows[:, 4 * quad : 4 * quad + 4, :])
+        for a in range(2):
             load_words(a)
-        bias = laid.tile([P, 1], F32, name="bias", align_bytes=64, offset=12288)
-        nc.sync.dma_start(bias[:], b.rearrange("(p o) -> p o", o=1))
+        nc.vector.memset(warm[:], 0.0)
+        for first in (32, 96):
+            nc.vector.memset(rows[first : first + 32, :], 0)
+            nc.vector.memset(planes[first : first + 32, :], 0)
+        nc.scalar.activation(warmed[:], warm[:], SILU)
+
         for g in range(2):
-            for u in range(2):
-                turned_row = turned[u][:].rearrange("n p c -> n (p c)")
-                for a in range(2):
-                    start = P * (2 * g + a)
-                    nc.tensor.transpose(second[g][:, a, u], turned_row[:, start : start + P], ident[:])
-            grouped_words = grouped[g][:].rearrange("p a n j -> p (a n j)").bitcast(F32).rearrange("p (a n u) -> p a n u", a=2, u=2)
-            nc.scalar.copy(grouped_words, second[g][:].rearrange("p a u n -> p a n u"))
+            nc.scalar.copy(grouped[g][:], raw[:, 2 * g : 2 * g + 2].rearrange("p a j n -> p a n j"))
             nc.vector.quantize_mx(
                 out=codes[g][:].rearrange("p a n -> p (a n)").bitcast(FP8X4),
                 scales=scales[g][:].rearrange("p a n -> p (a n)"),
                 in_=grouped[g][:].rearrange("p a n j -> p (a n j)"),
             )
-        for a in range(2):
-            nc.vector.tensor_copy(picked[a][:], words[a][:].bitcast(U32).indirect(offsets[:]))
-        picked_scales = held.tile([P, S], U8, name="picked_scales", tag="words1", align_bytes=64)
-        nc.vector.tensor_copy(picked_scales[:], packed[:].bitcast(U8).indirect(offsets[:]))
-        picked[2] = held.tile([P, S], U32, name="picked2", tag="packed", align_bytes=64)
+        words[2] = held.tile([P, T], I32, name="words2", tag="raw", align_bytes=64)
+        load_words(2)
+
+        gather_words(0)
+        picked_rows = held.tile([P, S], U8, name="picked_rows", tag="words0", align_bytes=64)
+        nc.vector.tensor_copy(picked_rows[:], rows[:].bitcast(U8).indirect(offsets[:]))
+        picked_view = picked_rows[:].bitcast(I32)
+        for first in (0, 64):
+            nc.sync.dma_start(planes[first + 32 : first + 48, :], picked_view[first + 16 : first + 32, :])
+            nc.vector.tensor_copy(planes[first : first + 32, :], picked_view[first : first + 32, :])
+        words[3] = laid.tile([P, T], I32, name="words3", align_bytes=64, offset=4032)
+        load_words(3)
+        bias = laid.tile([P, 1], F32, name="bias", align_bytes=64, offset=3072)
+        nc.sync.dma_start(bias[:], b.rearrange("(p o) -> p o", o=1))
+        picked[1] = laid.tile([P, S], U32, name="picked1", align_bytes=64, offset=64)
+        gather_words(1)
+        picked[2] = held.tile([P, S], U32, name="picked2", tag="words1", align_bytes=64)
+        gather_words(2)
         for a in range(PASSES):
-            window = words[a][:].bitcast(U32)
-            if a == 2:
-                nc.vector.tensor_copy(picked[a][:], window.indirect(offsets[:]))
             for h in range(2):
                 if a == PASSES - 1:
-                    cols = slice(h * HALF, (h + 1) * HALF)
-                    nc.vector.tensor_copy(picked[a][:, cols], window.indirect(offsets[:, h * HALF // 16 : (h + 1) * HALF // 16]))
+                    gather_words(a, h)
                 for c in (2 * h, 2 * h + 1):
                     multiply(a, c)
 

@@ -36,7 +36,7 @@ def tile_list_tabw_silu_kernel(tc, tab, w, b, offs, out):
         codes = [held.tile([P, 2, M], U32, name=f"codes{g}", align_bytes=64) for g in range(2)]
         scales = [held.tile([P, 2, M], U8, name=f"scales{g}", align_bytes=64) for g in range(2)]
 
-        raw = held.tile([P, PASSES, 4, M], F32, name="raw", tag="raw", align_bytes=64)
+        raw = [laid.tile([P, 2, 4, M], F32, name="raw0", align_bytes=64, offset=16384)]
         rows = laid.tile([P, T // 4], I32, name="rows", align_bytes=64, offset=2048)
         words = {0: held.tile([P, T], I32, name="words0", tag="words0", align_bytes=64)}
         words[1] = held.tile([P, T], I32, name="words1", tag="words1", align_bytes=64)
@@ -44,6 +44,18 @@ def tile_list_tabw_silu_kernel(tc, tab, w, b, offs, out):
 
         def load_words(a):
             nc.sync.dma_start(words[a][:], tab[a, 0 : 512 * T].bitcast(I32).rearrange("(p t) -> p t", p=P))
+
+        def load_weights(g):
+            part = w[1024 * g : 1024 * (g + 1), :]
+            nc.sync.dma_start(raw[g][:].rearrange("p a j n -> p a (j n)"), part.rearrange("(a p j) n -> p a (j n)", p=P, j=4))
+
+        def quantise_weights(g):
+            nc.scalar.copy(grouped[g][:], raw[g][:].rearrange("p a j n -> p a n j"))
+            nc.vector.quantize_mx(
+                out=codes[g][:].rearrange("p a n -> p (a n)").bitcast(FP8X4),
+                scales=scales[g][:].rearrange("p a n -> p (a n)"),
+                in_=grouped[g][:].rearrange("p a n j -> p (a n j)"),
+            )
 
         def gather_words(a, h=None):
             cols = slice(0, S) if h is None else slice(h * HALF, (h + 1) * HALF)
@@ -63,7 +75,7 @@ def tile_list_tabw_silu_kernel(tc, tab, w, b, offs, out):
             )
 
         scale_rows = tab[:, 512 * T : 528 * T].bitcast(I32).rearrange("a (q t) -> a q t", q=16)
-        nc.sync.dma_start(raw[:].rearrange("p a j n -> p a (j n)"), w.rearrange("(a p j) n -> p a (j n)", p=P, j=4))
+        load_weights(0)
         nc.sync.dma_start(offsets[:], offs)
         for quad in range(4):
             first = 64 * (quad // 2) + 16 * (quad % 2)
@@ -76,14 +88,10 @@ def tile_list_tabw_silu_kernel(tc, tab, w, b, offs, out):
             nc.vector.memset(planes[first : first + 32, :], 0)
         nc.scalar.activation(warmed[:], warm[:], SILU)
 
-        for g in range(2):
-            nc.scalar.copy(grouped[g][:], raw[:, 2 * g : 2 * g + 2].rearrange("p a j n -> p a n j"))
-            nc.vector.quantize_mx(
-                out=codes[g][:].rearrange("p a n -> p (a n)").bitcast(FP8X4),
-                scales=scales[g][:].rearrange("p a n -> p (a n)"),
-                in_=grouped[g][:].rearrange("p a n j -> p (a n j)"),
-            )
-        words[2] = held.tile([P, T], I32, name="words2", tag="raw", align_bytes=64)
+        quantise_weights(0)
+        raw.append(laid.tile([P, 2, 4, M], F32, name="raw1", align_bytes=64, offset=12352))
+        load_weights(1)
+        words[2] = laid.tile([P, T], I32, name="words2", align_bytes=64, offset=20416)
         load_words(2)
 
         gather_words(0)
@@ -99,6 +107,7 @@ def tile_list_tabw_silu_kernel(tc, tab, w, b, offs, out):
         nc.sync.dma_start(bias[:], b.rearrange("(p o) -> p o", o=1))
         picked[1] = laid.tile([P, S], U32, name="picked1", align_bytes=64, offset=64)
         gather_words(1)
+        quantise_weights(1)
         picked[2] = held.tile([P, S], U32, name="picked2", tag="words1", align_bytes=64)
         gather_words(2)
         for a in range(PASSES):

@@ -32,11 +32,12 @@ def tile_list_tabw_silu_kernel(tc, tab, w, b, offs, out):
         planes = held.tile([P, S // 4], I32, name="planes", align_bytes=64)
         acc = [psum.tile([P, PIECE], F32, name=f"acc{c}") for c in range(S // PIECE)]
         result = [held.tile([P, PIECE], F32, name=f"result{c}", align_bytes=64) for c in range(S // PIECE)]
-        grouped = [held.tile([P, 2, M, 4], BF16, name=f"grouped{g}", align_bytes=64) for g in range(2)]
+        grouped = [laid.tile([P, 2, M, 4], BF16, name="grouped0", align_bytes=64, offset=16384)]
+        grouped.append(held.tile([P, 2, M, 4], BF16, name="grouped1", align_bytes=64))
         codes = [held.tile([P, 2, M], U32, name=f"codes{g}", align_bytes=64) for g in range(2)]
         scales = [held.tile([P, 2, M], U8, name=f"scales{g}", align_bytes=64) for g in range(2)]
 
-        raw = [laid.tile([P, 2, 4, M], F32, name="raw0", align_bytes=64, offset=16384)]
+        raw = [held.tile([P, 2, 4, M], F32, name="raw0", align_bytes=64)]
         rows = laid.tile([P, T // 4], I32, name="rows", align_bytes=64, offset=2048)
         words = {0: held.tile([P, T], I32, name="words0", tag="words0", align_bytes=64)}
         words[1] = held.tile([P, T], I32, name="words1", tag="words1", align_bytes=64)
@@ -91,7 +92,7 @@ def tile_list_tabw_silu_kernel(tc, tab, w, b, offs, out):
         quantise_weights(0)
         raw.append(laid.tile([P, 2, 4, M], F32, name="raw1", align_bytes=64, offset=12352))
         load_weights(1)
-        words[2] = laid.tile([P, T], I32, name="words2", align_bytes=64, offset=20416)
+        words[2] = laid.tile([P, T], I32, name="words2", align_bytes=64, offset=18368)
         load_words(2)
 
         gather_words(0)

@@ -32,12 +32,11 @@ def tile_list_tabw_silu_kernel(tc, tab, w, b, offs, out):
         planes = held.tile([P, S // 4], I32, name="planes", align_bytes=64)
         acc = [psum.tile([P, PIECE], F32, name=f"acc{c}") for c in range(S // PIECE)]
         result = [held.tile([P, PIECE], F32, name=f"result{c}", align_bytes=64) for c in range(S // PIECE)]
-        grouped = [laid.tile([P, 2, M, 4], BF16, name="grouped0", align_bytes=64, offset=16384)]
-        grouped.append(held.tile([P, 2, M, 4], BF16, name="grouped1", align_bytes=64))
-        codes = [held.tile([P, 2, M], U32, name=f"codes{g}", align_bytes=64) for g in range(2)]
-        scales = [held.tile([P, 2, M], U8, name=f"scales{g}", align_bytes=64) for g in range(2)]
+        grouped = [held.tile([P, M, 4], BF16, name=f"grouped{a}", align_bytes=64) for a in range(PASSES)]
+        codes = [held.tile([P, M], U32, name=f"codes{a}", align_bytes=64) for a in range(PASSES)]
+        scales = [held.tile([P, M], U8, name=f"scales{a}", align_bytes=64) for a in range(PASSES)]
 
-        raw = [held.tile([P, 2, 4, M], F32, name="raw0", align_bytes=64)]
+        raw_first = laid.tile([P, 1, 4, M], F32, name="raw_first", align_bytes=64, offset=18368)
         rows = laid.tile([P, T // 4], I32, name="rows", align_bytes=64, offset=2048)
         words = {0: held.tile([P, T], I32, name="words0", tag="words0", align_bytes=64)}
         words[1] = held.tile([P, T], I32, name="words1", tag="words1", align_bytes=64)
@@ -46,16 +45,15 @@ def tile_list_tabw_silu_kernel(tc, tab, w, b, offs, out):
         def load_words(a):
             nc.sync.dma_start(words[a][:], tab[a, 0 : 512 * T].bitcast(I32).rearrange("(p t) -> p t", p=P))
 
-        def load_weights(g):
-            part = w[1024 * g : 1024 * (g + 1), :]
-            nc.sync.dma_start(raw[g][:].rearrange("p a j n -> p a (j n)"), part.rearrange("(a p j) n -> p a (j n)", p=P, j=4))
+        def load_weights(raw, rows_of_w):
+            nc.sync.dma_start(raw[:].rearrange("p a j n -> p a (j n)"), rows_of_w.rearrange("(a p j) n -> p a (j n)", p=P, j=4))
 
-        def quantise_weights(g):
-            nc.scalar.copy(grouped[g][:], raw[g][:].rearrange("p a j n -> p a n j"))
+        def quantise_weights(a, raw_pass):
+            nc.scalar.copy(grouped[a][:], raw_pass.rearrange("p j n -> p n j"))
             nc.vector.quantize_mx(
-                out=codes[g][:].rearrange("p a n -> p (a n)").bitcast(FP8X4),
-                scales=scales[g][:].rearrange("p a n -> p (a n)"),
-                in_=grouped[g][:].rearrange("p a n j -> p (a n j)"),
+                out=codes[a][:].bitcast(FP8X4),
+                scales=scales[a][:],
+                in_=grouped[a][:].rearrange("p n j -> p (n j)"),
             )
 
         def gather_words(a, h=None):
@@ -67,8 +65,8 @@ def tile_list_tabw_silu_kernel(tc, tab, w, b, offs, out):
             cols = slice(c * PIECE, (c + 1) * PIECE)
             nc.tensor.matmul_mx(
                 out=acc[c][:],
-                lhsT=codes[a // 2][:, a % 2].bitcast(FP8X4),
-                lhsT_scale=scales[a // 2][:, a % 2],
+                lhsT=codes[a][:].bitcast(FP8X4),
+                lhsT_scale=scales[a][:],
                 rhs=picked[a][:, cols].bitcast(FP8X4),
                 rhs_scale=planes[:].bitcast(U8)[4 * a :, cols],
                 start=(a == 0),
@@ -76,23 +74,23 @@ def tile_list_tabw_silu_kernel(tc, tab, w, b, offs, out):
             )
 
         scale_rows = tab[:, 512 * T : 528 * T].bitcast(I32).rearrange("a (q t) -> a q t", q=16)
-        load_weights(0)
+        load_words(0)
+        load_weights(raw_first, w[:512, :])
         nc.sync.dma_start(offsets[:], offs)
+        load_words(1)
         for quad in range(4):
             first = 64 * (quad // 2) + 16 * (quad % 2)
             nc.gpsimd.dma_start(rows[first : first + 16, :], scale_rows[:, 4 * quad : 4 * quad + 4, :])
-        for a in range(2):
-            load_words(a)
         nc.vector.memset(warm[:], 0.0)
         for first in (32, 96):
             nc.vector.memset(rows[first : first + 32, :], 0)
             nc.vector.memset(planes[first : first + 32, :], 0)
         nc.scalar.activation(warmed[:], warm[:], SILU)
 
-        quantise_weights(0)
-        raw.append(laid.tile([P, 2, 4, M], F32, name="raw1", align_bytes=64, offset=12352))
-        load_weights(1)
-        words[2] = laid.tile([P, T], I32, name="words2", align_bytes=64, offset=18368)
+        quantise_weights(0, raw_first[:, 0])
+        raw_rest = laid.tile([P, PASSES - 1, 4, M], F32, name="raw_rest", align_bytes=64, offset=12288)
+        load_weights(raw_rest, w[512:, :])
+        words[2] = laid.tile([P, T], I32, name="words2", align_bytes=64, offset=20352)
         load_words(2)
 
         gather_words(0)
@@ -108,7 +106,8 @@ def tile_list_tabw_silu_kernel(tc, tab, w, b, offs, out):
         nc.sync.dma_start(bias[:], b.rearrange("(p o) -> p o", o=1))
         picked[1] = laid.tile([P, S], U32, name="picked1", align_bytes=64, offset=64)
         gather_words(1)
-        quantise_weights(1)
+        for a in range(1, PASSES):
+            quantise_weights(a, raw_rest[:, a - 1])
         picked[2] = held.tile([P, S], U32, name="picked2", tag="words1", align_bytes=64)
         gather_words(2)
         for a in range(PASSES):

@@ -32,66 +32,72 @@ def tile_list_tabw_silu_kernel(tc, tab, w, b, offs, out):
         planes = held.tile([P, S // 4], I32, name="planes", align_bytes=64)
         acc = [psum.tile([P, PIECE], F32, name=f"acc{c}") for c in range(S // PIECE)]
         result = [held.tile([P, PIECE], F32, name=f"result{c}", align_bytes=64) for c in range(S // PIECE)]
-        grouped = [held.tile([P, M, 4], BF16, name=f"grouped{a}", align_bytes=64) for a in range(PASSES)]
-        codes = [held.tile([P, M], U32, name=f"codes{a}", align_bytes=64) for a in range(PASSES)]
-        scales = [held.tile([P, M], U8, name=f"scales{a}", align_bytes=64) for a in range(PASSES)]
+        raw = held.tile([P, 16, M], F32, name="raw", align_bytes=64)
+        identity = held.tile([P, P], F32, name="identity", align_bytes=64)
+        grouped = held.tile([P, PASSES * M * 4], BF16, name="grouped", align_bytes=64)
 
-        raw_first = laid.tile([P, 1, 4, M], F32, name="raw_first", align_bytes=64, offset=18368)
-        rows = laid.tile([P, T // 4], I32, name="rows", align_bytes=64, offset=2048)
+        zeros = laid.tile([P, P], F32, name="zeros", align_bytes=64, offset=7936)
+        rows = laid.tile([P, T // 4], I32, name="rows", align_bytes=64, offset=18432)
         words = {0: held.tile([P, T], I32, name="words0", tag="words0", align_bytes=64)}
-        words[1] = held.tile([P, T], I32, name="words1", tag="words1", align_bytes=64)
-        picked = {a: held.tile([P, S], U32, name=f"picked{a}", align_bytes=64) for a in (0, 3)}
+        picked = {a: held.tile([P, S], U32, name=f"picked{a}", align_bytes=64) for a in (0, 2, 3)}
 
         def load_words(a):
             nc.sync.dma_start(words[a][:], tab[a, 0 : 512 * T].bitcast(I32).rearrange("(p t) -> p t", p=P))
-
-        def load_weights(raw, rows_of_w):
-            nc.sync.dma_start(raw[:].rearrange("p a j n -> p a (j n)"), rows_of_w.rearrange("(a p j) n -> p a (j n)", p=P, j=4))
-
-        def quantise_weights(a, raw_pass):
-            nc.scalar.copy(grouped[a][:], raw_pass.rearrange("p j n -> p n j"))
-            nc.vector.quantize_mx(
-                out=codes[a][:].bitcast(FP8X4),
-                scales=scales[a][:],
-                in_=grouped[a][:].rearrange("p n j -> p (n j)"),
-            )
 
         def gather_words(a, h=None):
             cols = slice(0, S) if h is None else slice(h * HALF, (h + 1) * HALF)
             listed = offsets[:, cols.start // 16 : cols.stop // 16]
             nc.vector.tensor_copy(picked[a][:, cols], words[a][:].bitcast(U32).indirect(listed))
 
-        def multiply(a, c):
-            cols = slice(c * PIECE, (c + 1) * PIECE)
-            nc.tensor.matmul_mx(
-                out=acc[c][:],
-                lhsT=codes[a][:].bitcast(FP8X4),
-                lhsT_scale=scales[a][:],
-                rhs=picked[a][:, cols].bitcast(FP8X4),
-                rhs_scale=planes[:].bitcast(U8)[4 * a :, cols],
-                start=(a == 0),
-                stop=(a == PASSES - 1),
-            )
-
         scale_rows = tab[:, 512 * T : 528 * T].bitcast(I32).rearrange("a (q t) -> a q t", q=16)
-        load_words(0)
-        load_weights(raw_first, w[:512, :])
+        nc.sync.dma_start(raw[:].rearrange("p x n -> p (x n)"), w.rearrange("(p x) n -> p (x n)", p=P))
         nc.sync.dma_start(offsets[:], offs)
-        load_words(1)
+        load_words(0)
         for quad in range(4):
             first = 64 * (quad // 2) + 16 * (quad % 2)
             nc.gpsimd.dma_start(rows[first : first + 16, :], scale_rows[:, 4 * quad : 4 * quad + 4, :])
         nc.vector.memset(warm[:], 0.0)
+        nc.vector.memset(zeros[:], 0.0)
+        nc.gpsimd.affine_select(
+            out=identity[:],
+            in_=zeros[:],
+            compare_op=mybir.AluOpType.not_equal,
+            fill=1.0,
+            base=0,
+            pattern=[[-1, P]],
+            channel_multiplier=1,
+        )
         for first in (32, 96):
-            nc.vector.memset(rows[first : first + 32, :], 0)
-            nc.vector.memset(planes[first : first + 32, :], 0)
+            nc.gpsimd.memset(rows[first : first + 32, :], 0)
+        for first in (32, 96):
+            nc.gpsimd.memset(planes[first : first + 32, :], 0)
         nc.scalar.activation(warmed[:], warm[:], SILU)
 
-        quantise_weights(0, raw_first[:, 0])
-        raw_rest = laid.tile([P, PASSES - 1, 4, M], F32, name="raw_rest", align_bytes=64, offset=12288)
-        load_weights(raw_rest, w[512:, :])
-        words[2] = laid.tile([P, T], I32, name="words2", align_bytes=64, offset=20352)
+        words[1] = laid.tile([P, T], I32, name="words1", align_bytes=64, offset=0)
+        load_words(1)
+        words[2] = laid.tile([P, T], I32, name="words2", align_bytes=64, offset=8192)
         load_words(2)
+
+        by_pair = raw[:].rearrange("p (c u e) n -> p u c n e", u=2, e=2)
+        middle = []
+        for u in range(2):
+            pairs = held.tile([P, 4, M, 2], BF16, name=f"pairs{u}", align_bytes=64)
+            nc.scalar.copy(pairs[:], by_pair[:, u])
+            pair_words = pairs[:].rearrange("p c n e -> p (c n e)").bitcast(F32)
+            turned = psum.tile([P, 4, P], F32, name=f"turned{u}")
+            for c in range(4):
+                nc.tensor.transpose(turned[:, c, :], pair_words[:, c * M : (c + 1) * M], identity[:])
+            middle.append((turned, held.tile([P, PASSES, 32, 4], F32, name=f"middle{u}", align_bytes=64)))
+        for turned, dealt in middle:
+            nc.scalar.copy(dealt[:], turned[:].rearrange("n c (a v) -> n a v c", a=PASSES))
+        grouped_words = grouped[:].bitcast(F32).rearrange("p (a n u) -> p a n u", a=PASSES, u=2)
+        for h in range(2):
+            back = psum.tile([P, 2, 2, M], F32, name=f"back{h}")
+            for a in range(2):
+                for u in range(2):
+                    source = middle[u][1][:, 2 * h + a].rearrange("n v c -> n (v c)")
+                    nc.tensor.transpose(back[:, a, u, :], source, identity[:])
+            nc.scalar.copy(grouped_words[:, 2 * h : 2 * h + 2], back[:].rearrange("p a u n -> p a n u"))
 
         gather_words(0)
         picked_rows = held.tile([P, S], U8, name="picked_rows", tag="words0", align_bytes=64)
@@ -100,16 +106,29 @@ def tile_list_tabw_silu_kernel(tc, tab, w, b, offs, out):
         for first in (0, 64):
             nc.sync.dma_start(planes[first + 32 : first + 48, :], picked_view[first + 16 : first + 32, :])
             nc.vector.tensor_copy(planes[first : first + 32, :], picked_view[first : first + 32, :])
-        words[3] = laid.tile([P, T], I32, name="words3", align_bytes=64, offset=4032)
+        words[3] = laid.tile([P, T], I32, name="words3", align_bytes=64, offset=20416)
         load_words(3)
-        bias = laid.tile([P, 1], F32, name="bias", align_bytes=64, offset=3072)
+        bias = laid.tile([P, 1], F32, name="bias", align_bytes=64, offset=19456)
         nc.sync.dma_start(bias[:], b.rearrange("(p o) -> p o", o=1))
-        picked[1] = laid.tile([P, S], U32, name="picked1", align_bytes=64, offset=64)
+        picked[1] = laid.tile([P, S], U32, name="picked1", align_bytes=64, offset=16448)
         gather_words(1)
-        for a in range(1, PASSES):
-            quantise_weights(a, raw_rest[:, a - 1])
-        picked[2] = held.tile([P, S], U32, name="picked2", tag="words1", align_bytes=64)
+        codes = laid.tile([P, PASSES * M], U32, name="codes", align_bytes=64, offset=0)
+        scales = held.tile([P, PASSES * M], U8, name="scales", align_bytes=64)
+        nc.vector.quantize_mx(out=codes[:].bitcast(FP8X4), scales=scales[:], in_=grouped[:])
         gather_words(2)
+
+        def multiply(a, c):
+            cols = slice(c * PIECE, (c + 1) * PIECE)
+            nc.tensor.matmul_mx(
+                out=acc[c][:],
+                lhsT=codes[:, a * M : (a + 1) * M].bitcast(FP8X4),
+                lhsT_scale=scales[:, a * M : (a + 1) * M],
+                rhs=picked[a][:, cols].bitcast(FP8X4),
+                rhs_scale=planes[:].bitcast(U8)[4 * a :, cols],
+                start=(a == 0),
+                stop=(a == PASSES - 1),
+            )
+
         for a in range(PASSES):
             for h in range(2):
                 if a == PASSES - 1:

@@ -1,12 +1,14 @@
 from contextlib import ExitStack
 
 import concourse.mybir as mybir
+from concourse.masks import make_identity
 
 K, M, T, S = 2048, 128, 2048, 512
 P = 128
 PASSES = 4
 HALF = 256
 PIECE = 128
+EARLY = 768
 FLOPS = 2 * K * M * S
 
 F32 = mybir.dt.float32
@@ -32,57 +34,51 @@ def tile_list_tabw_silu_kernel(tc, tab, w, b, offs, out):
         planes = held.tile([P, S // 4], I32, name="planes", align_bytes=64)
         acc = [psum.tile([P, PIECE], F32, name=f"acc{c}") for c in range(S // PIECE)]
         result = [held.tile([P, PIECE], F32, name=f"result{c}", align_bytes=64) for c in range(S // PIECE)]
-        raw = held.tile([P, 16, M], F32, name="raw", align_bytes=64)
         identity = held.tile([P, P], F32, name="identity", align_bytes=64)
-        grouped = held.tile([P, PASSES * M * 4], BF16, name="grouped", align_bytes=64)
+        grouped = [held.tile([P, 2 * M * 4], BF16, name=f"grouped{h}", align_bytes=64) for h in range(2)]
 
-        zeros = laid.tile([P, P], F32, name="zeros", align_bytes=64, offset=7936)
+        raw = laid.tile([P, 16, M], F32, name="raw", align_bytes=64, offset=0)
         rows = laid.tile([P, T // 4], I32, name="rows", align_bytes=64, offset=18432)
-        words = {0: held.tile([P, T], I32, name="words0", tag="words0", align_bytes=64)}
+        shared = held.tile([P, 2 * T], I32, name="shared", align_bytes=64)
+        words = {0: shared[:, EARLY : EARLY + T], 1: shared[:, :T], 2: shared[:, T:]}
         picked = {a: held.tile([P, S], U32, name=f"picked{a}", align_bytes=64) for a in (0, 2, 3)}
 
-        def load_words(a):
-            nc.sync.dma_start(words[a][:], tab[a, 0 : 512 * T].bitcast(I32).rearrange("(p t) -> p t", p=P))
+        def load_words(a, cols=slice(0, T)):
+            nc.sync.dma_start(words[a][:, cols], tab[a, 0 : 512 * T].bitcast(I32).rearrange("(p t) -> p t", p=P)[:, cols])
 
         def gather_words(a, h=None):
             cols = slice(0, S) if h is None else slice(h * HALF, (h + 1) * HALF)
             listed = offsets[:, cols.start // 16 : cols.stop // 16]
-            nc.vector.tensor_copy(picked[a][:, cols], words[a][:].bitcast(U32).indirect(listed))
+            nc.vector.tensor_copy(picked[a][:, cols], words[a].bitcast(U32).indirect(listed))
 
         scale_rows = tab[:, 512 * T : 528 * T].bitcast(I32).rearrange("a (q t) -> a q t", q=16)
-        nc.sync.dma_start(raw[:].rearrange("p x n -> p (x n)"), w.rearrange("(p x) n -> p (x n)", p=P))
-        nc.sync.dma_start(offsets[:], offs)
         load_words(0)
+        nc.sync.dma_start(offsets[:], offs)
+        nc.sync.dma_start(raw[:].rearrange("p x n -> p (x n)"), w.rearrange("(p x) n -> p (x n)", p=P))
+        load_words(1, slice(0, EARLY))
         for quad in range(4):
             first = 64 * (quad // 2) + 16 * (quad % 2)
             nc.gpsimd.dma_start(rows[first : first + 16, :], scale_rows[:, 4 * quad : 4 * quad + 4, :])
         nc.vector.memset(warm[:], 0.0)
-        nc.vector.memset(zeros[:], 0.0)
-        nc.gpsimd.affine_select(
-            out=identity[:],
-            in_=zeros[:],
-            compare_op=mybir.AluOpType.not_equal,
-            fill=1.0,
-            base=0,
-            pattern=[[-1, P]],
-            channel_multiplier=1,
-        )
         for first in (32, 96):
-            nc.gpsimd.memset(rows[first : first + 32, :], 0)
-        for first in (32, 96):
-            nc.gpsimd.memset(planes[first : first + 32, :], 0)
+            nc.vector.memset(rows[first : first + 32, :], 0)
+            nc.vector.memset(planes[first : first + 32, :], 0)
+        nc.vector.memset(identity[:], 0.0)
+        make_identity(nc, identity[:], nomemset=True)
         nc.scalar.activation(warmed[:], warm[:], SILU)
 
-        words[1] = laid.tile([P, T], I32, name="words1", align_bytes=64, offset=0)
-        load_words(1)
-        words[2] = laid.tile([P, T], I32, name="words2", align_bytes=64, offset=8192)
+        gather_words(0)
+        load_words(1, slice(EARLY, T))
         load_words(2)
 
         by_pair = raw[:].rearrange("p (c u e) n -> p u c n e", u=2, e=2)
         middle = []
         for u in range(2):
             pairs = held.tile([P, 4, M, 2], BF16, name=f"pairs{u}", align_bytes=64)
-            nc.scalar.copy(pairs[:], by_pair[:, u])
+            if u == 0:
+                nc.vector.tensor_copy(pairs[:], by_pair[:, u])
+            else:
+                nc.scalar.copy(pairs[:], by_pair[:, u])
             pair_words = pairs[:].rearrange("p c n e -> p (c n e)").bitcast(F32)
             turned = psum.tile([P, 4, P], F32, name=f"turned{u}")
             for c in range(4):
@@ -90,31 +86,33 @@ def tile_list_tabw_silu_kernel(tc, tab, w, b, offs, out):
             middle.append((turned, held.tile([P, PASSES, 32, 4], F32, name=f"middle{u}", align_bytes=64)))
         for turned, dealt in middle:
             nc.scalar.copy(dealt[:], turned[:].rearrange("n c (a v) -> n a v c", a=PASSES))
-        grouped_words = grouped[:].bitcast(F32).rearrange("p (a n u) -> p a n u", a=PASSES, u=2)
         for h in range(2):
             back = psum.tile([P, 2, 2, M], F32, name=f"back{h}")
             for a in range(2):
                 for u in range(2):
                     source = middle[u][1][:, 2 * h + a].rearrange("n v c -> n (v c)")
                     nc.tensor.transpose(back[:, a, u, :], source, identity[:])
-            nc.scalar.copy(grouped_words[:, 2 * h : 2 * h + 2], back[:].rearrange("p a u n -> p a n u"))
+            grouped_words = grouped[h][:].bitcast(F32).rearrange("p (a n u) -> p a n u", a=2, u=2)
+            nc.scalar.copy(grouped_words, back[:].rearrange("p a u n -> p a n u"))
 
-        gather_words(0)
-        picked_rows = held.tile([P, S], U8, name="picked_rows", tag="words0", align_bytes=64)
+        picked_rows = laid.tile([P, S], U8, name="picked_rows", align_bytes=64, offset=0)
         nc.vector.tensor_copy(picked_rows[:], rows[:].bitcast(U8).indirect(offsets[:]))
         picked_view = picked_rows[:].bitcast(I32)
         for first in (0, 64):
             nc.sync.dma_start(planes[first + 32 : first + 48, :], picked_view[first + 16 : first + 32, :])
             nc.vector.tensor_copy(planes[first : first + 32, :], picked_view[first : first + 32, :])
-        words[3] = laid.tile([P, T], I32, name="words3", align_bytes=64, offset=20416)
+        last_words = laid.tile([P, T], I32, name="last_words", align_bytes=64, offset=20416)
+        words[3] = last_words[:]
         load_words(3)
         bias = laid.tile([P, 1], F32, name="bias", align_bytes=64, offset=19456)
         nc.sync.dma_start(bias[:], b.rearrange("(p o) -> p o", o=1))
         picked[1] = laid.tile([P, S], U32, name="picked1", align_bytes=64, offset=16448)
         gather_words(1)
-        codes = laid.tile([P, PASSES * M], U32, name="codes", align_bytes=64, offset=0)
+        codes = held.tile([P, PASSES * M], U32, name="codes", align_bytes=64)
         scales = held.tile([P, PASSES * M], U8, name="scales", align_bytes=64)
-        nc.vector.quantize_mx(out=codes[:].bitcast(FP8X4), scales=scales[:], in_=grouped[:])
+        for h in range(2):
+            cols = slice(2 * h * M, 2 * (h + 1) * M)
+            nc.vector.quantize_mx(out=codes[:, cols].bitcast(FP8X4), scales=scales[:, cols], in_=grouped[h][:])
         gather_words(2)
 
         def multiply(a, c):

@@ -35,13 +35,14 @@ def tile_list_tabw_silu_kernel(tc, tab, w, b, offs, out):
         acc = [psum.tile([P, PIECE], F32, name=f"acc{c}") for c in range(S // PIECE)]
         result = [held.tile([P, PIECE], F32, name=f"result{c}", align_bytes=64) for c in range(S // PIECE)]
         identity = held.tile([P, P], F32, name="identity", align_bytes=64)
-        grouped = [held.tile([P, 2 * M * 4], BF16, name=f"grouped{h}", align_bytes=64) for h in range(2)]
+        grouped = [held.tile([P, 2 * M * 4], BF16, name=f"grouped{h}", tag=f"grouped{h}", align_bytes=64) for h in range(2)]
 
         raw = laid.tile([P, 16, M], F32, name="raw", align_bytes=64, offset=0)
-        rows = laid.tile([P, T // 4], I32, name="rows", align_bytes=64, offset=18432)
+        last_words = held.tile([P, T], I32, name="last_words", align_bytes=64)
+        rows = last_words[:, T - T // 4 :]
         shared = held.tile([P, 2 * T], I32, name="shared", align_bytes=64)
-        words = {0: shared[:, EARLY : EARLY + T], 1: shared[:, :T], 2: shared[:, T:]}
-        picked = {a: held.tile([P, S], U32, name=f"picked{a}", align_bytes=64) for a in (0, 2, 3)}
+        words = [shared[:, T // 2 : T // 2 + T], shared[:, :T], shared[:, T:], last_words[:]]
+        picked = {a: held.tile([P, S], U32, name=f"picked{a}", align_bytes=64) for a in (0, 1, 3)}
 
         def load_words(a, cols=slice(0, T)):
             nc.sync.dma_start(words[a][:, cols], tab[a, 0 : 512 * T].bitcast(I32).rearrange("(p t) -> p t", p=P)[:, cols])
@@ -55,7 +56,7 @@ def tile_list_tabw_silu_kernel(tc, tab, w, b, offs, out):
         load_words(0)
         nc.sync.dma_start(offsets[:], offs)
         nc.sync.dma_start(raw[:].rearrange("p x n -> p (x n)"), w.rearrange("(p x) n -> p (x n)", p=P))
-        load_words(1, slice(0, EARLY))
+        load_words(3, slice(0, EARLY))
         for quad in range(4):
             first = 64 * (quad // 2) + 16 * (quad % 2)
             nc.gpsimd.dma_start(rows[first : first + 16, :], scale_rows[:, 4 * quad : 4 * quad + 4, :])
@@ -68,51 +69,49 @@ def tile_list_tabw_silu_kernel(tc, tab, w, b, offs, out):
         nc.scalar.activation(warmed[:], warm[:], SILU)
 
         gather_words(0)
-        load_words(1, slice(EARLY, T))
+        load_words(1)
         load_words(2)
 
         by_pair = raw[:].rearrange("p (c u e) n -> p u c n e", u=2, e=2)
-        middle = []
+        turned = [psum.tile([P, 4, P], F32, name=f"turned{u}", tag=f"turned{u}") for u in range(2)]
         for u in range(2):
-            pairs = held.tile([P, 4, M, 2], BF16, name=f"pairs{u}", align_bytes=64)
-            if u == 0:
-                nc.vector.tensor_copy(pairs[:], by_pair[:, u])
-            else:
-                nc.scalar.copy(pairs[:], by_pair[:, u])
-            pair_words = pairs[:].rearrange("p c n e -> p (c n e)").bitcast(F32)
-            turned = psum.tile([P, 4, P], F32, name=f"turned{u}")
-            for c in range(4):
-                nc.tensor.transpose(turned[:, c, :], pair_words[:, c * M : (c + 1) * M], identity[:])
-            middle.append((turned, held.tile([P, PASSES, 32, 4], F32, name=f"middle{u}", align_bytes=64)))
-        for turned, dealt in middle:
-            nc.scalar.copy(dealt[:], turned[:].rearrange("n c (a v) -> n a v c", a=PASSES))
-        for h in range(2):
-            back = psum.tile([P, 2, 2, M], F32, name=f"back{h}")
-            for a in range(2):
-                for u in range(2):
-                    source = middle[u][1][:, 2 * h + a].rearrange("n v c -> n (v c)")
-                    nc.tensor.transpose(back[:, a, u, :], source, identity[:])
-            grouped_words = grouped[h][:].bitcast(F32).rearrange("p (a n u) -> p a n u", a=2, u=2)
-            nc.scalar.copy(grouped_words, back[:].rearrange("p a u n -> p a n u"))
+            for g in range(2):
+                pairs = held.tile([P, 2, M, 2], BF16, name=f"pairs{u}{g}", align_bytes=64)
+                if (u, g) == (0, 1):
+                    nc.scalar.copy(pairs[:], by_pair[:, u, 2 * g : 2 * g + 2])
+                else:
+                    nc.vector.tensor_copy(pairs[:], by_pair[:, u, 2 * g : 2 * g + 2])
+                pair_words = pairs[:].rearrange("p c n e -> p (c n e)").bitcast(F32)
+                for c in range(2):
+                    nc.tensor.transpose(turned[u][:, 2 * g + c, :], pair_words[:, c * M : (c + 1) * M], identity[:])
+        middle = {}
+        for u in range(2):
+            for h in range(2):
+                middle[u, h] = held.tile([P, 2, 32, 4], F32, name=f"middle{u}{h}", tag=f"middle{u}{h}", align_bytes=64)
+                nc.scalar.copy(middle[u, h][:], turned[u][:].rearrange("n c (a v) -> n a v c", a=PASSES)[:, 2 * h : 2 * h + 2])
+        for a in range(PASSES):
+            back = psum.tile([P, 2, M], F32, name=f"back{a}", tag=f"back{a}" if a < 2 else f"turned{a - 2}")
+            for u in range(2):
+                nc.tensor.transpose(back[:, u, :], middle[u, a // 2][:, a % 2].rearrange("n v c -> n (v c)"), identity[:])
+            grouped_words = grouped[a // 2][:].bitcast(F32).rearrange("p (a n u) -> p a n u", a=2, u=2)
+            nc.scalar.copy(grouped_words[:, a % 2], back[:].rearrange("p u n -> p n u"))
 
         picked_rows = laid.tile([P, S], U8, name="picked_rows", align_bytes=64, offset=0)
-        nc.vector.tensor_copy(picked_rows[:], rows[:].bitcast(U8).indirect(offsets[:]))
+        nc.vector.tensor_copy(picked_rows[:], rows.bitcast(U8).indirect(offsets[:]))
         picked_view = picked_rows[:].bitcast(I32)
         for first in (0, 64):
             nc.sync.dma_start(planes[first + 32 : first + 48, :], picked_view[first + 16 : first + 32, :])
             nc.vector.tensor_copy(planes[first : first + 32, :], picked_view[first : first + 32, :])
-        last_words = laid.tile([P, T], I32, name="last_words", align_bytes=64, offset=20416)
-        words[3] = last_words[:]
-        load_words(3)
-        bias = laid.tile([P, 1], F32, name="bias", align_bytes=64, offset=19456)
+        load_words(3, slice(EARLY, T))
+        bias = held.tile([P, 1], F32, name="bias", tag="middle00", align_bytes=64)
         nc.sync.dma_start(bias[:], b.rearrange("(p o) -> p o", o=1))
-        picked[1] = laid.tile([P, S], U32, name="picked1", align_bytes=64, offset=16448)
         gather_words(1)
         codes = held.tile([P, PASSES * M], U32, name="codes", align_bytes=64)
         scales = held.tile([P, PASSES * M], U8, name="scales", align_bytes=64)
         for h in range(2):
             cols = slice(2 * h * M, 2 * (h + 1) * M)
             nc.vector.quantize_mx(out=codes[:, cols].bitcast(FP8X4), scales=scales[:, cols], in_=grouped[h][:])
+        picked[2] = held.tile([P, S], U32, name="picked2", tag="grouped1", align_bytes=64)
         gather_words(2)
 
         def multiply(a, c):

@@ -8,7 +8,7 @@ P = 128
 PASSES = 4
 HALF = 256
 PIECE = 128
-EARLY = 768
+EARLY = 896
 FLOPS = 2 * K * M * S
 
 F32 = mybir.dt.float32
@@ -25,41 +25,39 @@ def tile_list_tabw_silu_kernel(tc, tab, w, b, offs, out):
     nc = tc.nc
     with ExitStack() as ctx:
         held = ctx.enter_context(tc.tile_pool(name="held", bufs=1))
-        laid = ctx.enter_context(tc.tile_pool(name="laid", bufs=1))
         psum = ctx.enter_context(tc.psum_pool(name="psum", bufs=1))
 
         offsets = held.tile([P, S // 16], U16, name="offsets")
         warm = held.tile([P, 1], F32, name="warm")
         warmed = held.tile([P, 1], F32, name="warmed")
-        planes = held.tile([P, S // 4], I32, name="planes", align_bytes=64)
-        acc = [psum.tile([P, PIECE], F32, name=f"acc{c}") for c in range(S // PIECE)]
-        result = [held.tile([P, PIECE], F32, name=f"result{c}", align_bytes=64) for c in range(S // PIECE)]
         identity = held.tile([P, P], F32, name="identity", align_bytes=64)
-        grouped = [held.tile([P, 2 * M * 4], BF16, name=f"grouped{h}", tag=f"grouped{h}", align_bytes=64) for h in range(2)]
+        raw = held.tile([P, 16, M], F32, name="raw", tag="raw", align_bytes=64)
+        planes = held.tile([P, S // 4], I32, name="planes", align_bytes=64)
 
-        raw = laid.tile([P, 16, M], F32, name="raw", align_bytes=64, offset=0)
-        last_words = held.tile([P, T], I32, name="last_words", align_bytes=64)
-        rows = last_words[:, T - T // 4 :]
         shared = held.tile([P, 2 * T], I32, name="shared", align_bytes=64)
-        words = [shared[:, T // 2 : T // 2 + T], shared[:, :T], shared[:, T:], last_words[:]]
+        last = held.tile([P, T], I32, name="last", align_bytes=64)
+        rows = last[:, T - T // 4 :]
+        words = [shared[:, T // 2 : T // 2 + T], shared[:, :T], shared[:, T:], last[:]]
         picked = {a: held.tile([P, S], U32, name=f"picked{a}", align_bytes=64) for a in (0, 1, 3)}
 
         def load_words(a, cols=slice(0, T)):
-            nc.sync.dma_start(words[a][:, cols], tab[a, 0 : 512 * T].bitcast(I32).rearrange("(p t) -> p t", p=P)[:, cols])
+            in_hbm = tab[a, 0 : 512 * T].bitcast(I32).rearrange("(p t) -> p t", p=P)
+            nc.sync.dma_start(words[a][:, cols], in_hbm[:, cols])
 
-        def gather_words(a, h=None):
-            cols = slice(0, S) if h is None else slice(h * HALF, (h + 1) * HALF)
+        def gather_words(a, cols=slice(0, S)):
             listed = offsets[:, cols.start // 16 : cols.stop // 16]
             nc.vector.tensor_copy(picked[a][:, cols], words[a].bitcast(U32).indirect(listed))
 
-        scale_rows = tab[:, 512 * T : 528 * T].bitcast(I32).rearrange("a (q t) -> a q t", q=16)
         load_words(0)
         nc.sync.dma_start(offsets[:], offs)
         nc.sync.dma_start(raw[:].rearrange("p x n -> p (x n)"), w.rearrange("(p x) n -> p (x n)", p=P))
-        load_words(3, slice(0, EARLY))
+        load_words(PASSES - 1, slice(0, EARLY))
+
+        scale_rows = tab[:, 512 * T : 528 * T].bitcast(I32).rearrange("a (q t) -> a q t", q=16)
         for quad in range(4):
             first = 64 * (quad // 2) + 16 * (quad % 2)
             nc.gpsimd.dma_start(rows[first : first + 16, :], scale_rows[:, 4 * quad : 4 * quad + 4, :])
+
         nc.vector.memset(warm[:], 0.0)
         for first in (32, 96):
             nc.vector.memset(rows[first : first + 32, :], 0)
@@ -89,6 +87,7 @@ def tile_list_tabw_silu_kernel(tc, tab, w, b, offs, out):
             for h in range(2):
                 middle[u, h] = held.tile([P, 2, 32, 4], F32, name=f"middle{u}{h}", tag=f"middle{u}{h}", align_bytes=64)
                 nc.scalar.copy(middle[u, h][:], turned[u][:].rearrange("n c (a v) -> n a v c", a=PASSES)[:, 2 * h : 2 * h + 2])
+        grouped = [held.tile([P, 2 * M * 4], BF16, name=f"grouped{h}", tag=f"grouped{h}", align_bytes=64) for h in range(2)]
         for a in range(PASSES):
             back = psum.tile([P, 2, M], F32, name=f"back{a}", tag=f"back{a}" if a < 2 else f"turned{a - 2}")
             for u in range(2):
@@ -96,15 +95,16 @@ def tile_list_tabw_silu_kernel(tc, tab, w, b, offs, out):
             grouped_words = grouped[a // 2][:].bitcast(F32).rearrange("p (a n u) -> p a n u", a=2, u=2)
             nc.scalar.copy(grouped_words[:, a % 2], back[:].rearrange("p u n -> p n u"))
 
-        picked_rows = laid.tile([P, S], U8, name="picked_rows", align_bytes=64, offset=0)
+        picked_rows = held.tile([P, S], U8, name="picked_rows", tag="raw", align_bytes=64)
         nc.vector.tensor_copy(picked_rows[:], rows.bitcast(U8).indirect(offsets[:]))
         picked_view = picked_rows[:].bitcast(I32)
         for first in (0, 64):
             nc.sync.dma_start(planes[first + 32 : first + 48, :], picked_view[first + 16 : first + 32, :])
             nc.vector.tensor_copy(planes[first : first + 32, :], picked_view[first : first + 32, :])
-        load_words(3, slice(EARLY, T))
+        load_words(PASSES - 1, slice(EARLY, T))
         bias = held.tile([P, 1], F32, name="bias", tag="middle00", align_bytes=64)
         nc.sync.dma_start(bias[:], b.rearrange("(p o) -> p o", o=1))
+
         gather_words(1)
         codes = held.tile([P, PASSES * M], U32, name="codes", align_bytes=64)
         scales = held.tile([P, PASSES * M], U8, name="scales", align_bytes=64)
@@ -114,25 +114,24 @@ def tile_list_tabw_silu_kernel(tc, tab, w, b, offs, out):
         picked[2] = held.tile([P, S], U32, name="picked2", tag="grouped1", align_bytes=64)
         gather_words(2)
 
-        def multiply(a, c):
-            cols = slice(c * PIECE, (c + 1) * PIECE)
-            nc.tensor.matmul_mx(
-                out=acc[c][:],
-                lhsT=codes[:, a * M : (a + 1) * M].bitcast(FP8X4),
-                lhsT_scale=scales[:, a * M : (a + 1) * M],
-                rhs=picked[a][:, cols].bitcast(FP8X4),
-                rhs_scale=planes[:].bitcast(U8)[4 * a :, cols],
-                start=(a == 0),
-                stop=(a == PASSES - 1),
-            )
-
+        acc = [psum.tile([P, PIECE], F32, name=f"acc{c}") for c in range(S // PIECE)]
         for a in range(PASSES):
-            for h in range(2):
+            for first in range(0, S, HALF):
                 if a == PASSES - 1:
-                    gather_words(a, h)
-                for c in (2 * h, 2 * h + 1):
-                    multiply(a, c)
+                    gather_words(a, slice(first, first + HALF))
+                for c in range(first // PIECE, (first + HALF) // PIECE):
+                    cols = slice(c * PIECE, (c + 1) * PIECE)
+                    nc.tensor.matmul_mx(
+                        out=acc[c][:],
+                        lhsT=codes[:, a * M : (a + 1) * M].bitcast(FP8X4),
+                        lhsT_scale=scales[:, a * M : (a + 1) * M],
+                        rhs=picked[a][:, cols].bitcast(FP8X4),
+                        rhs_scale=planes[:].bitcast(U8)[4 * a :, cols],
+                        start=(a == 0),
+                        stop=(a == PASSES - 1),
+                    )
 
         for c in range(S // PIECE):
-            nc.scalar.activation(result[c][:], acc[c][:], SILU, bias=bias[:])
-            nc.sync.dma_start(out[:, c * PIECE : (c + 1) * PIECE], result[c][:])
+            result = held.tile([P, PIECE], F32, name=f"result{c}", align_bytes=64)
+            nc.scalar.activation(result[:], acc[c][:], SILU, bias=bias[:])
+            nc.sync.dma_start(out[:, c * PIECE : (c + 1) * PIECE], result[:])

@@ -8,7 +8,8 @@ P = 128
 PASSES = 4
 HALF = 256
 PIECE = 128
-EARLY = 896
+EARLY = 640
+DMA_ALIGN = 256
 FLOPS = 2 * K * M * S
 
 F32 = mybir.dt.float32
@@ -31,11 +32,11 @@ def tile_list_tabw_silu_kernel(tc, tab, w, b, offs, out):
         warm = held.tile([P, 1], F32, name="warm")
         warmed = held.tile([P, 1], F32, name="warmed")
         identity = held.tile([P, P], F32, name="identity", align_bytes=64)
-        raw = held.tile([P, 16, M], F32, name="raw", tag="raw", align_bytes=64)
-        planes = held.tile([P, S // 4], I32, name="planes", align_bytes=64)
+        raw = held.tile([P, 16, M], F32, name="raw", tag="raw", align_bytes=DMA_ALIGN)
+        planes = held.tile([P, S // 4], I32, name="planes", align_bytes=DMA_ALIGN)
 
-        shared = held.tile([P, 2 * T], I32, name="shared", align_bytes=64)
-        last = held.tile([P, T], I32, name="last", align_bytes=64)
+        shared = held.tile([P, 2 * T], I32, name="shared", align_bytes=DMA_ALIGN)
+        last = held.tile([P, T], I32, name="last", align_bytes=DMA_ALIGN)
         rows = last[:, T - T // 4 :]
         words = [shared[:, T // 2 : T // 2 + T], shared[:, :T], shared[:, T:], last[:]]
         picked = {a: held.tile([P, S], U32, name=f"picked{a}", align_bytes=64) for a in (0, 1, 3)}
@@ -95,7 +96,7 @@ def tile_list_tabw_silu_kernel(tc, tab, w, b, offs, out):
             grouped_words = grouped[a // 2][:].bitcast(F32).rearrange("p (a n u) -> p a n u", a=2, u=2)
             nc.scalar.copy(grouped_words[:, a % 2], back[:].rearrange("p u n -> p n u"))
 
-        picked_rows = held.tile([P, S], U8, name="picked_rows", tag="raw", align_bytes=64)
+        picked_rows = held.tile([P, S], U8, name="picked_rows", tag="raw", align_bytes=DMA_ALIGN)
         nc.vector.tensor_copy(picked_rows[:], rows.bitcast(U8).indirect(offsets[:]))
         picked_view = picked_rows[:].bitcast(I32)
         for first in (0, 64):
@@ -132,6 +133,6 @@ def tile_list_tabw_silu_kernel(tc, tab, w, b, offs, out):
                     )
 
         for c in range(S // PIECE):
-            result = held.tile([P, PIECE], F32, name=f"result{c}", align_bytes=64)
+            result = held.tile([P, PIECE], F32, name=f"result{c}", align_bytes=DMA_ALIGN)
             nc.scalar.activation(result[:], acc[c][:], SILU, bias=bias[:])
             nc.sync.dma_start(out[:, c * PIECE : (c + 1) * PIECE], result[:])

@@ -1,14 +1,13 @@
 from contextlib import ExitStack
 
 import concourse.mybir as mybir
-from concourse.masks import make_identity
 
 K, M, T, S = 2048, 128, 2048, 512
 P = 128
 PASSES = 4
 HALF = 256
 PIECE = 128
-EARLY = 640
+EARLY = 384
 DMA_ALIGN = 256
 FLOPS = 2 * K * M * S
 
@@ -29,17 +28,13 @@ def tile_list_tabw_silu_kernel(tc, tab, w, b, offs, out):
         psum = ctx.enter_context(tc.psum_pool(name="psum", bufs=1))
 
         offsets = held.tile([P, S // 16], U16, name="offsets")
-        warm = held.tile([P, 1], F32, name="warm")
-        warmed = held.tile([P, 1], F32, name="warmed")
-        identity = held.tile([P, P], F32, name="identity", align_bytes=64)
-        raw = held.tile([P, 16, M], F32, name="raw", tag="raw", align_bytes=DMA_ALIGN)
+        raw = held.tile([P, PASSES, 4, M], F32, name="raw", align_bytes=DMA_ALIGN)
         planes = held.tile([P, S // 4], I32, name="planes", align_bytes=DMA_ALIGN)
 
-        shared = held.tile([P, 2 * T], I32, name="shared", align_bytes=DMA_ALIGN)
-        last = held.tile([P, T], I32, name="last", align_bytes=DMA_ALIGN)
-        rows = last[:, T - T // 4 :]
-        words = [shared[:, T // 2 : T // 2 + T], shared[:, :T], shared[:, T:], last[:]]
-        picked = {a: held.tile([P, S], U32, name=f"picked{a}", align_bytes=64) for a in (0, 1, 3)}
+        shared = held.tile([P, 3 * T], I32, name="shared", align_bytes=DMA_ALIGN)
+        rows = shared[:, 3 * T - T // 4 :]
+        words = [shared[:, T // 2 : T // 2 + T], shared[:, :T], shared[:, T : 2 * T], shared[:, 2 * T :]]
+        picked = {a: held.tile([P, S], U32, name=f"picked{a}", align_bytes=64) for a in range(PASSES)}
 
         def load_words(a, cols=slice(0, T)):
             in_hbm = tab[a, 0 : 512 * T].bitcast(I32).rearrange("(p t) -> p t", p=P)
@@ -51,68 +46,44 @@ def tile_list_tabw_silu_kernel(tc, tab, w, b, offs, out):
 
         load_words(0)
         nc.sync.dma_start(offsets[:], offs)
-        nc.sync.dma_start(raw[:].rearrange("p x n -> p (x n)"), w.rearrange("(p x) n -> p (x n)", p=P))
-        load_words(PASSES - 1, slice(0, EARLY))
+        nc.sync.dma_start(
+            raw[:].rearrange("p a i n -> p a (i n)"), w.rearrange("(a p i) n -> p a (i n)", a=PASSES, i=4)
+        )
+        odd_passes = tab[1::2, 0 : 512 * T].bitcast(I32).rearrange("a (p t) -> p a t", p=P)
+        nc.sync.dma_start(shared[:].rearrange("p (a t) -> p a t", t=T)[:, 0::2, :EARLY], odd_passes[:, :, :EARLY])
+        bias = held.tile([P, 1], F32, name="bias")
+        nc.sync.dma_start(bias[:], b.rearrange("(p o) -> p o", o=1))
 
         scale_rows = tab[:, 512 * T : 528 * T].bitcast(I32).rearrange("a (q t) -> a q t", q=16)
         for quad in range(4):
             first = 64 * (quad // 2) + 16 * (quad % 2)
             nc.gpsimd.dma_start(rows[first : first + 16, :], scale_rows[:, 4 * quad : 4 * quad + 4, :])
 
-        nc.vector.memset(warm[:], 0.0)
         for first in (32, 96):
             nc.vector.memset(rows[first : first + 32, :], 0)
             nc.vector.memset(planes[first : first + 32, :], 0)
-        nc.vector.memset(identity[:], 0.0)
-        make_identity(nc, identity[:], nomemset=True)
-        nc.scalar.activation(warmed[:], warm[:], SILU)
 
         gather_words(0)
-        load_words(1)
+        load_words(1, slice(EARLY, T))
         load_words(2)
 
-        by_pair = raw[:].rearrange("p (c u e) n -> p u c n e", u=2, e=2)
-        turned = [psum.tile([P, 4, P], F32, name=f"turned{u}", tag=f"turned{u}") for u in range(2)]
-        for u in range(2):
-            for g in range(2):
-                pairs = held.tile([P, 2, M, 2], BF16, name=f"pairs{u}{g}", align_bytes=64)
-                if (u, g) == (0, 1):
-                    nc.scalar.copy(pairs[:], by_pair[:, u, 2 * g : 2 * g + 2])
-                else:
-                    nc.vector.tensor_copy(pairs[:], by_pair[:, u, 2 * g : 2 * g + 2])
-                pair_words = pairs[:].rearrange("p c n e -> p (c n e)").bitcast(F32)
-                for c in range(2):
-                    nc.tensor.transpose(turned[u][:, 2 * g + c, :], pair_words[:, c * M : (c + 1) * M], identity[:])
-        middle = {}
-        for u in range(2):
-            for h in range(2):
-                middle[u, h] = held.tile([P, 2, 32, 4], F32, name=f"middle{u}{h}", tag=f"middle{u}{h}", align_bytes=64)
-                nc.scalar.copy(middle[u, h][:], turned[u][:].rearrange("n c (a v) -> n a v c", a=PASSES)[:, 2 * h : 2 * h + 2])
-        grouped = [held.tile([P, 2 * M * 4], BF16, name=f"grouped{h}", tag=f"grouped{h}", align_bytes=64) for h in range(2)]
-        for a in range(PASSES):
-            back = psum.tile([P, 2, M], F32, name=f"back{a}", tag=f"back{a}" if a < 2 else f"turned{a - 2}")
-            for u in range(2):
-                nc.tensor.transpose(back[:, u, :], middle[u, a // 2][:, a % 2].rearrange("n v c -> n (v c)"), identity[:])
-            grouped_words = grouped[a // 2][:].bitcast(F32).rearrange("p (a n u) -> p a n u", a=2, u=2)
-            nc.scalar.copy(grouped_words[:, a % 2], back[:].rearrange("p u n -> p n u"))
+        grouped = held.tile([P, PASSES, M, 4], BF16, name="grouped", align_bytes=64)
+        nc.scalar.copy(grouped[:], raw[:].rearrange("p a i n -> p a n i"))
 
-        picked_rows = held.tile([P, S], U8, name="picked_rows", tag="raw", align_bytes=DMA_ALIGN)
+        picked_rows = held.tile([P, S], U8, name="picked_rows", tag="picked_rows", align_bytes=DMA_ALIGN)
         nc.vector.tensor_copy(picked_rows[:], rows.bitcast(U8).indirect(offsets[:]))
         picked_view = picked_rows[:].bitcast(I32)
         for first in (0, 64):
             nc.sync.dma_start(planes[first + 32 : first + 48, :], picked_view[first + 16 : first + 32, :])
             nc.vector.tensor_copy(planes[first : first + 32, :], picked_view[first : first + 32, :])
         load_words(PASSES - 1, slice(EARLY, T))
-        bias = held.tile([P, 1], F32, name="bias", tag="middle00", align_bytes=64)
-        nc.sync.dma_start(bias[:], b.rearrange("(p o) -> p o", o=1))
 
-        gather_words(1)
         codes = held.tile([P, PASSES * M], U32, name="codes", align_bytes=64)
         scales = held.tile([P, PASSES * M], U8, name="scales", align_bytes=64)
-        for h in range(2):
-            cols = slice(2 * h * M, 2 * (h + 1) * M)
-            nc.vector.quantize_mx(out=codes[:, cols].bitcast(FP8X4), scales=scales[:, cols], in_=grouped[h][:])
-        picked[2] = held.tile([P, S], U32, name="picked2", tag="grouped1", align_bytes=64)
+        nc.vector.quantize_mx(
+            out=codes[:].bitcast(FP8X4), scales=scales[:], in_=grouped[:].rearrange("p a n i -> p (a n i)")
+        )
+        gather_words(1)
         gather_words(2)
 
         acc = [psum.tile([P, PIECE], F32, name=f"acc{c}") for c in range(S // PIECE)]

@@ -5,9 +5,8 @@ import concourse.mybir as mybir
 K, M, T, S = 2048, 128, 2048, 512
 P = 128
 PASSES = 4
-HALF = 256
 PIECE = 128
-EARLY = 384
+EARLY = 704
 DMA_ALIGN = 256
 FLOPS = 2 * K * M * S
 
@@ -31,9 +30,10 @@ def tile_list_tabw_silu_kernel(tc, tab, w, b, offs, out):
         raw = held.tile([P, PASSES, 4, M], F32, name="raw", align_bytes=DMA_ALIGN)
         planes = held.tile([P, S // 4], I32, name="planes", align_bytes=DMA_ALIGN)
 
-        shared = held.tile([P, 3 * T], I32, name="shared", align_bytes=DMA_ALIGN)
-        rows = shared[:, 3 * T - T // 4 :]
-        words = [shared[:, T // 2 : T // 2 + T], shared[:, :T], shared[:, T : 2 * T], shared[:, 2 * T :]]
+        shared = held.tile([P, 2 * T], I32, name="shared", align_bytes=DMA_ALIGN)
+        final = held.tile([P, T], I32, name="final", align_bytes=DMA_ALIGN)
+        rows = final[:, T - T // 4 :]
+        words = [shared[:, T // 2 : T // 2 + T], shared[:, :T], shared[:, T:], final[:]]
         picked = {a: held.tile([P, S], U32, name=f"picked{a}", align_bytes=64) for a in range(PASSES)}
 
         def load_words(a, cols=slice(0, T)):
@@ -49,8 +49,7 @@ def tile_list_tabw_silu_kernel(tc, tab, w, b, offs, out):
         nc.sync.dma_start(
             raw[:].rearrange("p a i n -> p a (i n)"), w.rearrange("(a p i) n -> p a (i n)", a=PASSES, i=4)
         )
-        odd_passes = tab[1::2, 0 : 512 * T].bitcast(I32).rearrange("a (p t) -> p a t", p=P)
-        nc.sync.dma_start(shared[:].rearrange("p (a t) -> p a t", t=T)[:, 0::2, :EARLY], odd_passes[:, :, :EARLY])
+        load_words(PASSES - 1, slice(0, EARLY))
         bias = held.tile([P, 1], F32, name="bias")
         nc.sync.dma_start(bias[:], b.rearrange("(p o) -> p o", o=1))
 
@@ -64,7 +63,7 @@ def tile_list_tabw_silu_kernel(tc, tab, w, b, offs, out):
             nc.vector.memset(planes[first : first + 32, :], 0)
 
         gather_words(0)
-        load_words(1, slice(EARLY, T))
+        load_words(1)
         load_words(2)
 
         grouped = held.tile([P, PASSES, M, 4], BF16, name="grouped", align_bytes=64)
@@ -88,20 +87,19 @@ def tile_list_tabw_silu_kernel(tc, tab, w, b, offs, out):
 
         acc = [psum.tile([P, PIECE], F32, name=f"acc{c}") for c in range(S // PIECE)]
         for a in range(PASSES):
-            for first in range(0, S, HALF):
+            for c in range(S // PIECE):
+                cols = slice(c * PIECE, (c + 1) * PIECE)
                 if a == PASSES - 1:
-                    gather_words(a, slice(first, first + HALF))
-                for c in range(first // PIECE, (first + HALF) // PIECE):
-                    cols = slice(c * PIECE, (c + 1) * PIECE)
-                    nc.tensor.matmul_mx(
-                        out=acc[c][:],
-                        lhsT=codes[:, a * M : (a + 1) * M].bitcast(FP8X4),
-                        lhsT_scale=scales[:, a * M : (a + 1) * M],
-                        rhs=picked[a][:, cols].bitcast(FP8X4),
-                        rhs_scale=planes[:].bitcast(U8)[4 * a :, cols],
-                        start=(a == 0),
-                        stop=(a == PASSES - 1),
-                    )
+                    gather_words(a, cols)
+                nc.tensor.matmul_mx(
+                    out=acc[c][:],
+                    lhsT=codes[:, a * M : (a + 1) * M].bitcast(FP8X4),
+                    lhsT_scale=scales[:, a * M : (a + 1) * M],
+                    rhs=picked[a][:, cols].bitcast(FP8X4),
+                    rhs_scale=planes[:].bitcast(U8)[4 * a :, cols],
+                    start=(a == 0),
+                    stop=(a == PASSES - 1),
+                )
 
         for c in range(S // PIECE):
             result = held.tile([P, PIECE], F32, name=f"result{c}", align_bytes=DMA_ALIGN)

@@ -50,8 +50,6 @@ def tile_list_tabw_silu_kernel(tc, tab, w, b, offs, out):
             raw[:].rearrange("p a i n -> p a (i n)"), w.rearrange("(a p i) n -> p a (i n)", a=PASSES, i=4)
         )
         load_words(PASSES - 1, slice(0, EARLY))
-        bias = held.tile([P, 1], F32, name="bias")
-        nc.sync.dma_start(bias[:], b.rearrange("(p o) -> p o", o=1))
 
         scale_rows = tab[:, 512 * T : 528 * T].bitcast(I32).rearrange("a (q t) -> a q t", q=16)
         for quad in range(4):
@@ -69,6 +67,9 @@ def tile_list_tabw_silu_kernel(tc, tab, w, b, offs, out):
         grouped = held.tile([P, PASSES, M, 4], BF16, name="grouped", align_bytes=64)
         nc.scalar.copy(grouped[:], raw[:].rearrange("p a i n -> p a n i"))
 
+        unread = held.tile([P, 1], F32, name="unread")
+        nc.scalar.activation(unread[:], raw[:, 0, 0, 0:1], SILU)
+
         picked_rows = held.tile([P, S], U8, name="picked_rows", tag="picked_rows", align_bytes=DMA_ALIGN)
         nc.vector.tensor_copy(picked_rows[:], rows.bitcast(U8).indirect(offsets[:]))
         picked_view = picked_rows[:].bitcast(I32)
@@ -76,6 +77,8 @@ def tile_list_tabw_silu_kernel(tc, tab, w, b, offs, out):
             nc.sync.dma_start(planes[first + 32 : first + 48, :], picked_view[first + 16 : first + 32, :])
             nc.vector.tensor_copy(planes[first : first + 32, :], picked_view[first : first + 32, :])
         load_words(PASSES - 1, slice(EARLY, T))
+        bias = held.tile([P, 1], F32, name="bias", tag="picked_rows", align_bytes=DMA_ALIGN)
+        nc.sync.dma_start(bias[:], b.rearrange("(p o) -> p o", o=1))
 
         codes = held.tile([P, PASSES * M], U32, name="codes", align_bytes=64)
         scales = held.tile([P, PASSES * M], U8, name="scales", align_bytes=64)

@@ -6,7 +6,7 @@ K, M, T, S = 2048, 128, 2048, 512
 P = 128
 PASSES = 4
 PIECE = 128
-EARLY = 704
+EARLY = 832
 DMA_ALIGN = 256
 FLOPS = 2 * K * M * S
 

@@ -6,7 +6,7 @@ K, M, T, S = 2048, 128, 2048, 512
 P = 128
 PASSES = 4
 PIECE = 128
-EARLY = 832
+EARLY = 768
 DMA_ALIGN = 256
 FLOPS = 2 * K * M * S
 

from contextlib import ExitStack

import concourse.mybir as mybir

K, M, T, S = 2048, 128, 2048, 512
P = 128
PASSES = 4
PIECE = 128
EARLY = 768
DMA_ALIGN = 256
FLOPS = 2 * K * M * S

F32 = mybir.dt.float32
BF16 = mybir.dt.bfloat16
I32 = mybir.dt.int32
U32 = mybir.dt.uint32
U16 = mybir.dt.uint16
U8 = mybir.dt.uint8
FP8X4 = mybir.dt.float8_e4m3fn_x4
SILU = mybir.ActivationFunctionType.Silu


def tile_list_tabw_silu_kernel(tc, tab, w, b, offs, out):
    nc = tc.nc
    with ExitStack() as ctx:
        held = ctx.enter_context(tc.tile_pool(name="held", bufs=1))
        psum = ctx.enter_context(tc.psum_pool(name="psum", bufs=1))

        offsets = held.tile([P, S // 16], U16, name="offsets")
        raw = held.tile([P, PASSES, 4, M], F32, name="raw", align_bytes=DMA_ALIGN)
        planes = held.tile([P, S // 4], I32, name="planes", align_bytes=DMA_ALIGN)

        shared = held.tile([P, 2 * T], I32, name="shared", align_bytes=DMA_ALIGN)
        final = held.tile([P, T], I32, name="final", align_bytes=DMA_ALIGN)
        rows = final[:, T - T // 4 :]
        words = [shared[:, T // 2 : T // 2 + T], shared[:, :T], shared[:, T:], final[:]]
        picked = {a: held.tile([P, S], U32, name=f"picked{a}", align_bytes=64) for a in range(PASSES)}

        def load_words(a, cols=slice(0, T)):
            in_hbm = tab[a, 0 : 512 * T].bitcast(I32).rearrange("(p t) -> p t", p=P)
            nc.sync.dma_start(words[a][:, cols], in_hbm[:, cols])

        def gather_words(a, cols=slice(0, S)):
            listed = offsets[:, cols.start // 16 : cols.stop // 16]
            nc.vector.tensor_copy(picked[a][:, cols], words[a].bitcast(U32).indirect(listed))

        load_words(0)
        nc.sync.dma_start(offsets[:], offs)
        nc.sync.dma_start(
            raw[:].rearrange("p a i n -> p a (i n)"), w.rearrange("(a p i) n -> p a (i n)", a=PASSES, i=4)
        )
        load_words(PASSES - 1, slice(0, EARLY))

        scale_rows = tab[:, 512 * T : 528 * T].bitcast(I32).rearrange("a (q t) -> a q t", q=16)
        for quad in range(4):
            first = 64 * (quad // 2) + 16 * (quad % 2)
            nc.gpsimd.dma_start(rows[first : first + 16, :], scale_rows[:, 4 * quad : 4 * quad + 4, :])

        for first in (32, 96):
            nc.vector.memset(rows[first : first + 32, :], 0)
            nc.vector.memset(planes[first : first + 32, :], 0)

        gather_words(0)
        load_words(1)
        load_words(2)

        grouped = held.tile([P, PASSES, M, 4], BF16, name="grouped", align_bytes=64)
        nc.scalar.copy(grouped[:], raw[:].rearrange("p a i n -> p a n i"))

        unread = held.tile([P, 1], F32, name="unread")
        nc.scalar.activation(unread[:], raw[:, 0, 0, 0:1], SILU)

        picked_rows = held.tile([P, S], U8, name="picked_rows", tag="picked_rows", align_bytes=DMA_ALIGN)
        nc.vector.tensor_copy(picked_rows[:], rows.bitcast(U8).indirect(offsets[:]))
        picked_view = picked_rows[:].bitcast(I32)
        for first in (0, 64):
            nc.sync.dma_start(planes[first + 32 : first + 48, :], picked_view[first + 16 : first + 32, :])
            nc.vector.tensor_copy(planes[first : first + 32, :], picked_view[first : first + 32, :])
        load_words(PASSES - 1, slice(EARLY, T))
        bias = held.tile([P, 1], F32, name="bias", tag="picked_rows", align_bytes=DMA_ALIGN)
        nc.sync.dma_start(bias[:], b.rearrange("(p o) -> p o", o=1))

        codes = held.tile([P, PASSES * M], U32, name="codes", align_bytes=64)
        scales = held.tile([P, PASSES * M], U8, name="scales", align_bytes=64)
        nc.vector.quantize_mx(
            out=codes[:].bitcast(FP8X4), scales=scales[:], in_=grouped[:].rearrange("p a n i -> p (a n i)")
        )
        gather_words(1)
        gather_words(2)

        acc = [psum.tile([P, PIECE], F32, name=f"acc{c}") for c in range(S // PIECE)]
        for a in range(PASSES):
            for c in range(S // PIECE):
                cols = slice(c * PIECE, (c + 1) * PIECE)
                if a == PASSES - 1:
                    gather_words(a, cols)
                nc.tensor.matmul_mx(
                    out=acc[c][:],
                    lhsT=codes[:, a * M : (a + 1) * M].bitcast(FP8X4),
                    lhsT_scale=scales[:, a * M : (a + 1) * M],
                    rhs=picked[a][:, cols].bitcast(FP8X4),
                    rhs_scale=planes[:].bitcast(U8)[4 * a :, cols],
                    start=(a == 0),
                    stop=(a == PASSES - 1),
                )

        for c in range(S // PIECE):
            result = held.tile([P, PIECE], F32, name=f"result{c}", align_bytes=DMA_ALIGN)
            nc.scalar.activation(result[:], acc[c][:], SILU, bias=bias[:])
            nc.sync.dma_start(out[:, c * PIECE : (c + 1) * PIECE], result[:])
